import numpy as np
import ml_dtypes


def mxq(x, axis, fmt="e4m3"):
    dtype, down = {"e4m3": (ml_dtypes.float8_e4m3fn, 7), "e5m2": (ml_dtypes.float8_e5m2, 14)}[fmt]
    v = np.moveaxis(np.asarray(x, np.float32).astype(ml_dtypes.bfloat16).astype(np.float64), axis, -1)
    blocks = v.reshape(v.shape[:-1] + (-1, 32))
    amax = np.abs(blocks).max(-1, keepdims=True)
    byte = np.maximum(np.where(amax > 0, np.frexp(amax)[1] - 1 + 127, 0) - down, 1)
    scale = np.exp2(byte - 127.0)
    codes = (blocks / scale).astype(np.float32).astype(dtype).astype(np.float64)
    return np.moveaxis((codes * scale).reshape(v.shape), -1, axis)


WIDE = False


def mx_kscale(k):
    if not WIDE:
        return np.ones(k)
    levels = np.array([10, -10, 5, -5, 0])
    if k % 512:
        return np.exp2(np.random.permutation(np.resize(levels, k // 32))).repeat(32)
    a = np.empty((k // 512, 16))
    for p in range(k // 512):
        a[p, :8] = np.random.permutation(np.resize(levels, 8))
        for g in range(8):
            far = levels[np.abs(levels - a[p, g]) >= 10]
            a[p, g + 8] = far[np.random.randint(len(far))]
    return np.exp2(a.ravel()).repeat(32)


def f64(x):
    return np.asarray(x).astype(np.float64)


def striped(idx):
    return np.tile(idx.reshape(-1, 16).T, (8, 1)).astype(np.uint16)


def unstriped(offs):
    return offs[:16].T.reshape(-1).astype(np.int64)


E2M1 = np.array([0.0, 0.5, 1.0, 1.5, 2.0, 3.0, 4.0, 6.0, -0.0, -0.5, -1.0, -1.5, -2.0, -3.0, -4.0, -6.0])


def pack_fp4(w):
    k, n = w.shape
    w = f64(np.asarray(w, np.float32).astype(ml_dtypes.bfloat16)).reshape(k // 32, 32, n)
    amax = np.abs(w).max(1)
    mant, ex = np.frexp(amax / 6.0)
    byte = np.clip(np.where(amax > 0, np.where(mant > 0.5, ex, ex - 1) + 127, 1), 1, 254)
    scaled = (w * np.exp2(127.0 - byte)[:, None, :]).reshape(k, n).astype(np.float32)
    c = np.ascontiguousarray(scaled.reshape(k // 512, 128, 4, n).transpose(0, 1, 3, 2)).astype(ml_dtypes.float4_e2m1fn).view(np.uint8) & 0xF
    words = (c[..., 0::2] | (c[..., 1::2] << 4)).reshape(k // 512, 128, 2 * n)
    return np.ascontiguousarray(words), np.ascontiguousarray(byte.astype(np.uint8).reshape(k // 512, 16, n))


def unpack_fp4(words, scales):
    g, _, n = scales.shape
    words = np.ascontiguousarray(words).reshape(g, 128, n, 2)
    nib = np.empty((g, 128, n, 4), np.uint8)
    nib[..., 0::2] = words & 0xF
    nib[..., 1::2] = words >> 4
    vals = E2M1[nib] * np.repeat(np.exp2(scales.astype(np.float64) - 127.0), 8, axis=1)[..., None]
    return vals.transpose(0, 1, 3, 2).reshape(g * 512, n)


def sigmoid(v):
    return 1.0 / (1.0 + np.exp(-np.maximum(v, -700.0)))


K, T, S, N = 1024, 2048, 1024, 256


def setup_inputs():
    n = np.random.standard_normal
    s = mx_kscale(K)[:, None]
    packed_w1 = pack_fp4(n((K, N)) / np.sqrt(K) / s)
    return {
        "xT": (n((K, T)) * s).astype(np.float32),
        "side": n((N, T)).astype(np.float32),
        "w1_words": packed_w1[0],
        "w1_scales": packed_w1[1],
        "offs": striped(np.random.permutation(T)[:S]),
    }


def reference(xT, side, w1_words, w1_scales, offs):
    xq = mxq(f64(xT)[:, unstriped(offs)], 0, "e4m3")
    y = unpack_fp4(w1_words, w1_scales).T @ xq
    g = f64(side)[:, unstriped(offs)]
    return y * sigmoid(g)

@@ -1,0 +1,171 @@
+from contextlib import ExitStack
+
+import concourse.mybir as mybir
+
+K, T, S, N = 1024, 2048, 1024, 256
+FLOPS = 2 * K * S * N
+
+F32 = mybir.dt.float32
+BF16 = mybir.dt.bfloat16
+I32 = mybir.dt.int32
+U32 = mybir.dt.uint32
+U16 = mybir.dt.uint16
+U8 = mybir.dt.uint8
+FP8X4 = mybir.dt.float8_e4m3fn_x4
+FP4X4 = mybir.dt.float4_e2m1fn_x4
+
+P = 128
+K_PASS = 512
+BANK = 512
+LIST_ROWS = 16
+
+PAIRS = [
+    [(0, 2048, [(1344, "v"), (2048, "s")])],
+    [(0, 1024, [(1024, "s")]), (1024, 2048, [(1664, "v"), (2048, "s")])],
+    [(0, 1024, [(1024, "s")]), (1024, 2048, [(1664, "v"), (2048, "s")])],
+    [(0, 1024, [(1024, "s")]), (1024, 1536, [(1536, "v")]), (1536, 1792, [(1792, "v")]), (1792, 2048, [(2048, "v")])],
+]
+CHUNK = [512, 256]
+
+
+def tile_picked_sidegate_sigmoid_l_kernel(tc, xT, side, w1_words, w1_scales, offs, out):
+    nc = tc.nc
+    with ExitStack() as ctx:
+        keep = ctx.enter_context(tc.tile_pool(name="keep", bufs=1))
+        psum = ctx.enter_context(tc.psum_pool(name="psum", bufs=1))
+
+        offsets = keep.tile([P, S // LIST_ROWS], U16, name="offsets")
+        w_codes = keep.tile([P, 2, 2 * N], U8, name="w_codes", align_bytes=64)
+        w_scales = keep.tile([P, 2, N], U8, name="w_scales", align_bytes=64)
+
+        def entries(first, count):
+            return offsets[:, first // LIST_ROWS : (first + count) // LIST_ROWS]
+
+        side_rows = [keep.tile([P, T], F32, name=f"side_rows{b}") for b in range(2)]
+        nc.sync.dma_start(out=side_rows[0][:], in_=side[0:P, :])
+        nc.sync.dma_start(offsets[:], offs)
+
+        nc.vector.memset(w_scales[:].rearrange("p g n -> p (g n)").bitcast(I32), 0)
+        for q in range(4):
+            nc.scalar.dma_start(
+                out=w_scales[32 * q : 32 * q + 4, :, :].bitcast(I32),
+                in_=w1_scales[:, 4 * q : 4 * q + 4, :].rearrange("g r n -> r g n").bitcast(I32),
+            )
+
+        x_rows = xT.rearrange("(g p u e) t -> g u p e t", g=2, p=P, u=2, e=2)
+        raw = {}
+        for pair, loads in enumerate(PAIRS):
+            if pair == 2:
+                nc.sync.dma_start(out=side_rows[1][:], in_=side[P : 2 * P, :])
+            for first, end, casts in loads:
+                raw[pair, first] = keep.tile([P, 2, end - first], F32, name=f"raw{pair}_{first}", tag=f"raw{pair}_{first}")
+                nc.sync.dma_start(out=raw[pair, first][:], in_=x_rows[pair // 2, pair % 2, :, :, first:end])
+        nc.sync.dma_start(out=w_codes[:].bitcast(I32), in_=w1_words.rearrange("g p n -> p g n").bitcast(I32))
+
+        picked_side = [keep.tile([P, S], F32, name=f"picked_side{b}") for b in range(2)]
+        gates = {}
+
+        def gather_side(b):
+            nc.vector.tensor_copy(out=picked_side[b][:], in_=side_rows[b][:].indirect(offsets[:]))
+
+        def sigmoid(b, tag):
+            gates[b] = keep.tile([P, S], F32, name=f"gate{b}", tag=tag)
+            nc.scalar.activation(out=gates[b][:], in_=picked_side[b][:], func=mybir.ActivationFunctionType.Sigmoid)
+
+        windows = [keep.tile([P, T, 2], BF16, name=f"window{pair}") for pair in range(4)]
+
+        def cast(pair):
+            for first, end, casts in PAIRS[pair]:
+                lo = first
+                for hi, engine in casts:
+                    source = raw[pair, first][:, :, lo - first : hi - first].rearrange("p e t -> p t e")
+                    if engine == "v":
+                        nc.vector.tensor_copy(out=windows[pair][:, lo:hi, :], in_=source)
+                    else:
+                        nc.scalar.copy(out=windows[pair][:, lo:hi, :], in_=source)
+                    lo = hi
+
+        picked = {}
+        woven = {}
+        for g in range(2):
+            for c in range(S // CHUNK[g]):
+                picked[g, c] = keep.tile([P, 2, CHUNK[g]], U32, name=f"picked{g}_{c}")
+                woven[g, c] = keep.tile([P, CHUNK[g], 2], U32, name=f"woven{g}_{c}", align_bytes=64)
+        x_codes = {(g, h): keep.tile([P, BANK], U32, name=f"x_codes{g}_{h}", align_bytes=64) for g in range(2) for h in range(2)}
+        x_scales = {(g, h): keep.tile([P, BANK], U8, name=f"x_scales{g}_{h}", align_bytes=64) for g in range(2) for h in range(2)}
+        acc = {(b, h): psum.tile([P, BANK], F32, name=f"acc{b}_{h}") for b in range(2) for h in range(2)}
+
+        def gather(pair, c):
+            g, u = divmod(pair, 2)
+            words = windows[pair][:].rearrange("p t e -> p (t e)").bitcast(U32)
+            nc.vector.tensor_copy(out=picked[g, c][:, u, :], in_=words.indirect(entries(c * CHUNK[g], CHUNK[g])))
+
+        def weave(g, c):
+            nc.scalar.copy(out=woven[g, c][:], in_=picked[g, c][:].rearrange("p u j -> p j u"))
+
+        def quantize(g, c):
+            h, first = divmod(c * CHUNK[g], BANK)
+            cols = slice(first, first + CHUNK[g])
+            nc.vector.quantize_mx(
+                out=x_codes[g, h][:, cols].bitcast(FP8X4),
+                scales=x_scales[g, h][:, cols],
+                in_=woven[g, c][:].rearrange("p j u -> p (j u)").bitcast(BF16),
+            )
+
+        def multiply(g, b, h):
+            nc.tensor.matmul_mx(
+                out=acc[b, h][:],
+                lhsT=w_codes[:, g, 2 * P * b : 2 * P * (b + 1)].bitcast(FP4X4),
+                lhsT_scale=w_scales[:, g, P * b : P * (b + 1)],
+                rhs=x_codes[g, h][:].bitcast(FP8X4),
+                rhs_scale=x_scales[g, h][:],
+                start=(g == 0),
+                stop=(g == 1),
+            )
+
+        def finish(b, h):
+            cols = slice(h * BANK, (h + 1) * BANK)
+            result = keep.tile([P, BANK], F32, name=f"result{b}_{h}")
+            nc.vector.tensor_tensor(out=result[:], in0=acc[b, h][:], in1=gates[b][:, cols], op=mybir.AluOpType.mult)
+            nc.sync.dma_start(out=out[P * b : P * (b + 1), cols], in_=result[:])
+
+        gather_side(0)
+        sigmoid(0, "gate0")
+        cast(0)
+        for c in range(2):
+            gather(0, c)
+        cast(1)
+        for c in range(2):
+            gather(1, c)
+            weave(0, c)
+        gather_side(1)
+        quantize(0, 0)
+        quantize(0, 1)
+        cast(2)
+        sigmoid(1, "raw2_1024")
+        for c in range(4):
+            gather(2, c)
+        cast(3)
+        for h in range(2):
+            for b in range(2):
+                multiply(0, b, h)
+        gather(3, 0)
+        weave(1, 0)
+        gather(3, 1)
+        weave(1, 1)
+        quantize(1, 0)
+        gather(3, 2)
+        weave(1, 2)
+        quantize(1, 1)
+        multiply(1, 0, 0)
+        multiply(1, 1, 0)
+        gather(3, 3)
+        weave(1, 3)
+        quantize(1, 2)
+        finish(0, 0)
+        quantize(1, 3)
+        multiply(1, 0, 1)
+        multiply(1, 1, 1)
+        finish(1, 0)
+        finish(0, 1)
+        finish(1, 1)

@@ -21,9 +21,9 @@ LIST_ROWS = 16
 
 PAIRS = [
     [(0, 2048, [(1344, "v"), (2048, "s")])],
+    [(0, 1024, [(1024, "s")]), (1024, 2048, [(1696, "v"), (2048, "s")])],
     [(0, 1024, [(1024, "s")]), (1024, 2048, [(1664, "v"), (2048, "s")])],
-    [(0, 1024, [(1024, "s")]), (1024, 2048, [(1664, "v"), (2048, "s")])],
-    [(0, 1024, [(1024, "s")]), (1024, 1536, [(1536, "v")]), (1536, 1792, [(1792, "v")]), (1792, 2048, [(2048, "v")])],
+    [(0, 1024, [(1024, "s")]), (1024, 1664, [(1664, "v")]), (1664, 2048, [(1920, "v"), (2048, "s")])],
 ]
 CHUNK = [512, 256]
 
@@ -46,11 +46,6 @@ def tile_picked_sidegate_sigmoid_l_kernel(tc, xT, side, w1_words, w1_scales, off
         nc.sync.dma_start(offsets[:], offs)
 
         nc.vector.memset(w_scales[:].rearrange("p g n -> p (g n)").bitcast(I32), 0)
-        for q in range(4):
-            nc.scalar.dma_start(
-                out=w_scales[32 * q : 32 * q + 4, :, :].bitcast(I32),
-                in_=w1_scales[:, 4 * q : 4 * q + 4, :].rearrange("g r n -> r g n").bitcast(I32),
-            )
 
         x_rows = xT.rearrange("(g p u e) t -> g u p e t", g=2, p=P, u=2, e=2)
         raw = {}
@@ -60,6 +55,11 @@ def tile_picked_sidegate_sigmoid_l_kernel(tc, xT, side, w1_words, w1_scales, off
             for first, end, casts in loads:
                 raw[pair, first] = keep.tile([P, 2, end - first], F32, name=f"raw{pair}_{first}", tag=f"raw{pair}_{first}")
                 nc.sync.dma_start(out=raw[pair, first][:], in_=x_rows[pair // 2, pair % 2, :, :, first:end])
+        for q in range(4):
+            nc.sync.dma_start(
+                out=w_scales[32 * q : 32 * q + 4, :, :].bitcast(I32),
+                in_=w1_scales[:, 4 * q : 4 * q + 4, :].rearrange("g r n -> r g n").bitcast(I32),
+            )
         nc.sync.dma_start(out=w_codes[:].bitcast(I32), in_=w1_words.rearrange("g p n -> p g n").bitcast(I32))
 
         picked_side = [keep.tile([P, S], F32, name=f"picked_side{b}") for b in range(2)]
@@ -78,11 +78,12 @@ def tile_picked_sidegate_sigmoid_l_kernel(tc, xT, side, w1_words, w1_scales, off
             for first, end, casts in PAIRS[pair]:
                 lo = first
                 for hi, engine in casts:
-                    source = raw[pair, first][:, :, lo - first : hi - first].rearrange("p e t -> p t e")
+                    source = raw[pair, first][:, :, lo - first : hi - first].rearrange("p e (c i) -> p c e i", i=4)
+                    target = windows[pair][:, lo:hi, :].rearrange("p (c i) e -> p c e i", i=4)
                     if engine == "v":
-                        nc.vector.tensor_copy(out=windows[pair][:, lo:hi, :], in_=source)
+                        nc.vector.tensor_copy(out=target, in_=source)
                     else:
-                        nc.scalar.copy(out=windows[pair][:, lo:hi, :], in_=source)
+                        nc.scalar.copy(out=target, in_=source)
                     lo = hi
 
         picked = {}
@@ -101,7 +102,10 @@ def tile_picked_sidegate_sigmoid_l_kernel(tc, xT, side, w1_words, w1_scales, off
             nc.vector.tensor_copy(out=picked[g, c][:, u, :], in_=words.indirect(entries(c * CHUNK[g], CHUNK[g])))
 
         def weave(g, c):
-            nc.scalar.copy(out=woven[g, c][:], in_=picked[g, c][:].rearrange("p u j -> p j u"))
+            nc.scalar.copy(
+                out=woven[g, c][:].rearrange("p (j i) u -> p j u i", i=2),
+                in_=picked[g, c][:].rearrange("p u (j i) -> p j u i", i=2),
+            )
 
         def quantize(g, c):
             h, first = divmod(c * CHUNK[g], BANK)

@@ -15,21 +15,21 @@ FP8X4 = mybir.dt.float8_e4m3fn_x4
 FP4X4 = mybir.dt.float4_e2m1fn_x4
 
 P = 128
-K_PASS = 512
 BANK = 512
 LIST_ROWS = 16
 
 PAIRS = [
-    [(0, 2048, [(1344, "v"), (2048, "s")])],
-    [(0, 1024, [(1024, "s")]), (1024, 2048, [(1696, "v"), (2048, "s")])],
-    [(0, 1024, [(1024, "s")]), (1024, 2048, [(1664, "v"), (2048, "s")])],
+    [(0, 2048, [(1408, "v"), (2048, "s")])],
     [(0, 1024, [(1024, "s")]), (1024, 1664, [(1664, "v")]), (1664, 2048, [(1920, "v"), (2048, "s")])],
+    [(0, 512, [(512, "s")]), (512, 1280, [(1280, "v")]), (1280, 2048, [(1792, "v"), (2048, "s")])],
+    [(0, 512, [(512, "s")]), (512, 1152, [(1152, "s")]), (1152, 1792, [(1392, "s"), (1792, "v")]), (1792, 2048, [(1952, "v"), (2048, "s")])],
 ]
 CHUNK = [512, 256]
 
 
 def tile_picked_sidegate_sigmoid_l_kernel(tc, xT, side, w1_words, w1_scales, offs, out):
     nc = tc.nc
+    sigmoid = mybir.ActivationFunctionType.Sigmoid
     with ExitStack() as ctx:
         keep = ctx.enter_context(tc.tile_pool(name="keep", bufs=1))
         psum = ctx.enter_context(tc.psum_pool(name="psum", bufs=1))
@@ -41,41 +41,51 @@ def tile_picked_sidegate_sigmoid_l_kernel(tc, xT, side, w1_words, w1_scales, off
         def entries(first, count):
             return offsets[:, first // LIST_ROWS : (first + count) // LIST_ROWS]
 
-        side_rows = [keep.tile([P, T], F32, name=f"side_rows{b}") for b in range(2)]
-        nc.sync.dma_start(out=side_rows[0][:], in_=side[0:P, :])
-        nc.sync.dma_start(offsets[:], offs)
-
         nc.vector.memset(w_scales[:].rearrange("p g n -> p (g n)").bitcast(I32), 0)
+
+        warm = keep.tile([P, 16], F32, name="warm")
+        nc.vector.memset(warm[:, 0:8], 0.0)
+        nc.scalar.activation(out=warm[:, 8:16], in_=warm[:, 0:8], func=sigmoid)
 
         x_rows = xT.rearrange("(g p u e) t -> g u p e t", g=2, p=P, u=2, e=2)
         raw = {}
-        for pair, loads in enumerate(PAIRS):
-            if pair == 2:
-                nc.sync.dma_start(out=side_rows[1][:], in_=side[P : 2 * P, :])
-            for first, end, casts in loads:
-                raw[pair, first] = keep.tile([P, 2, end - first], F32, name=f"raw{pair}_{first}", tag=f"raw{pair}_{first}")
-                nc.sync.dma_start(out=raw[pair, first][:], in_=x_rows[pair // 2, pair % 2, :, :, first:end])
-        for q in range(4):
-            nc.sync.dma_start(
-                out=w_scales[32 * q : 32 * q + 4, :, :].bitcast(I32),
-                in_=w1_scales[:, 4 * q : 4 * q + 4, :].rearrange("g r n -> r g n").bitcast(I32),
-            )
-        nc.sync.dma_start(out=w_codes[:].bitcast(I32), in_=w1_words.rearrange("g p n -> p g n").bitcast(I32))
 
-        picked_side = [keep.tile([P, S], F32, name=f"picked_side{b}") for b in range(2)]
-        gates = {}
-
-        def gather_side(b):
-            nc.vector.tensor_copy(out=picked_side[b][:], in_=side_rows[b][:].indirect(offsets[:]))
-
-        def sigmoid(b, tag):
-            gates[b] = keep.tile([P, S], F32, name=f"gate{b}", tag=tag)
-            nc.scalar.activation(out=gates[b][:], in_=picked_side[b][:], func=mybir.ActivationFunctionType.Sigmoid)
-
-        windows = [keep.tile([P, T, 2], BF16, name=f"window{pair}") for pair in range(4)]
-
-        def cast(pair):
+        def load_pair(pair):
             for first, end, casts in PAIRS[pair]:
+                raw[pair, first] = keep.tile([P, 2, end - first], F32, name=f"raw{pair}_{first}", tag=f"raw{pair}_{first}", align_bytes=64)
+                nc.sync.dma_start(out=raw[pair, first][:], in_=x_rows[pair // 2, pair % 2, :, :, first:end])
+
+        def load_weights(queue):
+            for q in range(4):
+                queue.dma_start(
+                    out=w_scales[32 * q : 32 * q + 4, :, :].bitcast(I32),
+                    in_=w1_scales[:, 4 * q : 4 * q + 4, :].rearrange("g r n -> r g n").bitcast(I32),
+                )
+            queue.dma_start(out=w_codes[:].bitcast(I32), in_=w1_words.rearrange("g p n -> p g n").bitcast(I32))
+
+        side_rows = [keep.tile([P, T], F32, name=f"side_rows{b}") for b in range(2)]
+
+        def load_side(b):
+            nc.sync.dma_start(out=side_rows[b][:], in_=side[b * P : (b + 1) * P, :])
+
+        load_pair(0)
+        nc.sync.dma_start(offsets[:], offs)
+        load_pair(1)
+        load_pair(2)
+        load_pair(3)
+        load_weights(nc.sync)
+        load_side(0)
+        load_side(1)
+
+        windows = {}
+        window_tags = {}
+
+        def cast(pair, which=None):
+            if pair not in windows:
+                windows[pair] = keep.tile([P, T, 2], BF16, name=f"window{pair}", tag=window_tags.get(pair, f"window{pair}"))
+            for n, (first, end, casts) in enumerate(PAIRS[pair]):
+                if which is not None and n != which:
+                    continue
                 lo = first
                 for hi, engine in casts:
                     source = raw[pair, first][:, :, lo - first : hi - first].rearrange("p e (c i) -> p c e i", i=4)
@@ -86,13 +96,19 @@ def tile_picked_sidegate_sigmoid_l_kernel(tc, xT, side, w1_words, w1_scales, off
                         nc.scalar.copy(out=target, in_=source)
                     lo = hi
 
+        woven_pass = [keep.tile([P, S, 2], U32, name=f"woven{g}", tag=tag, align_bytes=64) for g, tag in enumerate(["raw2_0", "woven1"])]
         picked = {}
         woven = {}
         for g in range(2):
             for c in range(S // CHUNK[g]):
-                picked[g, c] = keep.tile([P, 2, CHUNK[g]], U32, name=f"picked{g}_{c}")
-                woven[g, c] = keep.tile([P, CHUNK[g], 2], U32, name=f"woven{g}_{c}", align_bytes=64)
-        x_codes = {(g, h): keep.tile([P, BANK], U32, name=f"x_codes{g}_{h}", align_bytes=64) for g in range(2) for h in range(2)}
+                picked[g, c] = keep.tile([P, 2, CHUNK[g]], U32, name=f"picked{g}_{c}", tag=f"picked{g}_{c}")
+                woven[g, c] = woven_pass[g][:, c * CHUNK[g] : (c + 1) * CHUNK[g], :]
+        code_tags = {}
+        x_codes = {
+            (g, h): keep.tile([P, BANK], U32, name=f"x_codes{g}_{h}", tag=code_tags.get((g, h), f"x_codes{g}_{h}"), align_bytes=64)
+            for g in range(2)
+            for h in range(2)
+        }
         x_scales = {(g, h): keep.tile([P, BANK], U8, name=f"x_scales{g}_{h}", align_bytes=64) for g in range(2) for h in range(2)}
         acc = {(b, h): psum.tile([P, BANK], F32, name=f"acc{b}_{h}") for b in range(2) for h in range(2)}
 
@@ -101,11 +117,13 @@ def tile_picked_sidegate_sigmoid_l_kernel(tc, xT, side, w1_words, w1_scales, off
             words = windows[pair][:].rearrange("p t e -> p (t e)").bitcast(U32)
             nc.vector.tensor_copy(out=picked[g, c][:, u, :], in_=words.indirect(entries(c * CHUNK[g], CHUNK[g])))
 
-        def weave(g, c):
-            nc.scalar.copy(
-                out=woven[g, c][:].rearrange("p (j i) u -> p j u i", i=2),
-                in_=picked[g, c][:].rearrange("p u (j i) -> p j u i", i=2),
-            )
+        def weave(g, c, engine="s"):
+            target = woven[g, c].rearrange("p (j i) u -> p j u i", i=2)
+            source = picked[g, c][:].rearrange("p u (j i) -> p j u i", i=2)
+            if engine == "v":
+                nc.vector.tensor_copy(out=target.bitcast(I32), in_=source.bitcast(I32))
+            else:
+                nc.scalar.copy(out=target, in_=source)
 
         def quantize(g, c):
             h, first = divmod(c * CHUNK[g], BANK)
@@ -113,7 +131,7 @@ def tile_picked_sidegate_sigmoid_l_kernel(tc, xT, side, w1_words, w1_scales, off
             nc.vector.quantize_mx(
                 out=x_codes[g, h][:, cols].bitcast(FP8X4),
                 scales=x_scales[g, h][:, cols],
-                in_=woven[g, c][:].rearrange("p j u -> p (j u)").bitcast(BF16),
+                in_=woven[g, c].rearrange("p j u -> p (j u)").bitcast(BF16),
             )
 
         def multiply(g, b, h):
@@ -127,49 +145,63 @@ def tile_picked_sidegate_sigmoid_l_kernel(tc, xT, side, w1_words, w1_scales, off
                 stop=(g == 1),
             )
 
-        def finish(b, h):
-            cols = slice(h * BANK, (h + 1) * BANK)
-            result = keep.tile([P, BANK], F32, name=f"result{b}_{h}")
-            nc.vector.tensor_tensor(out=result[:], in0=acc[b, h][:], in1=gates[b][:, cols], op=mybir.AluOpType.mult)
-            nc.sync.dma_start(out=out[P * b : P * (b + 1), cols], in_=result[:])
+        gates = keep.tile([P, 2 * S], F32, name="gates", tag="picked1_1")
 
-        gather_side(0)
-        sigmoid(0, "gate0")
+        def gate(b, first, count):
+            nc.scalar.activation(
+                out=gates[:, b * S + first : b * S + first + count], in_=side_rows[b][:].indirect(entries(first, count)), func=sigmoid
+            )
+
+        def finish(b, first, count, queue=nc.sync, tag=None):
+            h, inside = divmod(first, BANK)
+            result = keep.tile([P, count], F32, name=f"result{b}_{first}", tag=tag or f"result{b}_{first}")
+            nc.vector.tensor_tensor(
+                out=result[:], in0=acc[b, h][:, inside : inside + count], in1=gates[:, b * S + first : b * S + first + count], op=mybir.AluOpType.mult
+            )
+            queue.dma_start(out=out[P * b : P * (b + 1), first : first + count], in_=result[:])
+
         cast(0)
         for c in range(2):
             gather(0, c)
         cast(1)
-        for c in range(2):
-            gather(1, c)
-            weave(0, c)
-        gather_side(1)
+        gather(1, 0)
+        gather(1, 1)
+        cast(2, 0)
+        weave(0, 0)
+        weave(0, 1)
+        cast(2, 1)
         quantize(0, 0)
-        quantize(0, 1)
-        cast(2)
-        sigmoid(1, "raw2_1024")
+        cast(2, 2)
         for c in range(4):
             gather(2, c)
-        cast(3)
+        quantize(0, 1)
         for h in range(2):
             for b in range(2):
                 multiply(0, b, h)
+        cast(3)
         gather(3, 0)
         weave(1, 0)
         gather(3, 1)
         weave(1, 1)
-        quantize(1, 0)
         gather(3, 2)
-        weave(1, 2)
+        quantize(1, 0)
+        gather(3, 3)
         quantize(1, 1)
         multiply(1, 0, 0)
         multiply(1, 1, 0)
-        gather(3, 3)
-        weave(1, 3)
+        weave(1, 2, "v")
+        weave(1, 3, "v")
         quantize(1, 2)
-        finish(0, 0)
         quantize(1, 3)
         multiply(1, 0, 1)
         multiply(1, 1, 1)
-        finish(1, 0)
-        finish(0, 1)
-        finish(1, 1)
+        gate(0, 0, 512)
+        gate(0, 512, 512)
+        gate(1, 0, 512)
+        gate(1, 512, 256)
+        gate(1, 768, 256)
+        finish(0, 0, 512)
+        finish(0, 512, 512)
+        finish(1, 0, 512)
+        finish(1, 512, 256)
+        finish(1, 768, 256)

@@ -96,14 +96,17 @@ def tile_picked_sidegate_sigmoid_l_kernel(tc, xT, side, w1_words, w1_scales, off
                         nc.scalar.copy(out=target, in_=source)
                     lo = hi
 
-        woven_pass = [keep.tile([P, S, 2], U32, name=f"woven{g}", tag=tag, align_bytes=64) for g, tag in enumerate(["raw2_0", "woven1"])]
+        woven_first = keep.tile([P, S, 2], U32, name="woven0", tag="raw2_0", align_bytes=64)
         picked = {}
         woven = {}
         for g in range(2):
             for c in range(S // CHUNK[g]):
                 picked[g, c] = keep.tile([P, 2, CHUNK[g]], U32, name=f"picked{g}_{c}", tag=f"picked{g}_{c}")
-                woven[g, c] = woven_pass[g][:, c * CHUNK[g] : (c + 1) * CHUNK[g], :]
-        code_tags = {}
+                if g == 0:
+                    woven[g, c] = woven_first[:, c * CHUNK[g] : (c + 1) * CHUNK[g], :]
+                else:
+                    woven[g, c] = keep.tile([P, CHUNK[g], 2], U32, name=f"woven{g}_{c}", align_bytes=64)[:]
+        code_tags = {(0, 1): "raw2_1280"}
         x_codes = {
             (g, h): keep.tile([P, BANK], U32, name=f"x_codes{g}_{h}", tag=code_tags.get((g, h), f"x_codes{g}_{h}"), align_bytes=64)
             for g in range(2)
@@ -145,7 +148,7 @@ def tile_picked_sidegate_sigmoid_l_kernel(tc, xT, side, w1_words, w1_scales, off
                 stop=(g == 1),
             )
 
-        gates = keep.tile([P, 2 * S], F32, name="gates", tag="picked1_1")
+        gates = keep.tile([P, 2 * S], F32, name="gates", tag="picked1_0")
 
         def gate(b, first, count):
             nc.scalar.activation(
@@ -179,17 +182,15 @@ def tile_picked_sidegate_sigmoid_l_kernel(tc, xT, side, w1_words, w1_scales, off
             for b in range(2):
                 multiply(0, b, h)
         cast(3)
-        gather(3, 0)
+        for c in range(4):
+            gather(3, c)
         weave(1, 0)
-        gather(3, 1)
-        weave(1, 1)
-        gather(3, 2)
+        weave(1, 1, "v")
         quantize(1, 0)
-        gather(3, 3)
+        weave(1, 2, "v")
         quantize(1, 1)
         multiply(1, 0, 0)
         multiply(1, 1, 0)
-        weave(1, 2, "v")
         weave(1, 3, "v")
         quantize(1, 2)
         quantize(1, 3)

@@ -17,14 +17,21 @@ FP4X4 = mybir.dt.float4_e2m1fn_x4
 P = 128
 BANK = 512
 LIST_ROWS = 16
+MX_ALIGN = 64
 
-PAIRS = [
-    [(0, 2048, [(1408, "v"), (2048, "s")])],
-    [(0, 1024, [(1024, "s")]), (1024, 1664, [(1664, "v")]), (1664, 2048, [(1920, "v"), (2048, "s")])],
-    [(0, 512, [(512, "s")]), (512, 1280, [(1280, "v")]), (1280, 2048, [(1792, "v"), (2048, "s")])],
-    [(0, 512, [(512, "s")]), (512, 1152, [(1152, "s")]), (1152, 1792, [(1392, "s"), (1792, "v")]), (1792, 2048, [(1952, "v"), (2048, "s")])],
+PIECES = [
+    [(0, 1280, 480), (1280, T, 280)],
+    [(0, 1408, 688), (1408, T, 240)],
+    [(0, 512, 512), (512, 1280, 304), (1280, T, 304)],
+    [(0, 896, 896), (896, 1728, 416), (1728, T, 112)],
 ]
 CHUNK = [512, 256]
+SCALAR_WEAVES = 384
+WIDE_FIRST = [(0, 0, BANK), (1, 0, BANK)]
+NARROW = [(0, first, P) for first in range(BANK, S, P)]
+WIDE_LAST = [(1, BANK, BANK)]
+GROUPS = WIDE_FIRST + NARROW + WIDE_LAST
+OUTPUTS = [(0, 0, 512), (0, 512, 512), (1, 0, 512), (1, 512, 256), (1, 768, 256)]
 
 
 def tile_picked_sidegate_sigmoid_l_kernel(tc, xT, side, w1_words, w1_scales, offs, out):
@@ -35,8 +42,8 @@ def tile_picked_sidegate_sigmoid_l_kernel(tc, xT, side, w1_words, w1_scales, off
         psum = ctx.enter_context(tc.psum_pool(name="psum", bufs=1))
 
         offsets = keep.tile([P, S // LIST_ROWS], U16, name="offsets")
-        w_codes = keep.tile([P, 2, 2 * N], U8, name="w_codes", align_bytes=64)
-        w_scales = keep.tile([P, 2, N], U8, name="w_scales", align_bytes=64)
+        w_codes = keep.tile([P, 2, 2 * N], U8, name="w_codes", align_bytes=MX_ALIGN)
+        w_scales = keep.tile([P, 2, N], U8, name="w_scales", align_bytes=MX_ALIGN)
 
         def entries(first, count):
             return offsets[:, first // LIST_ROWS : (first + count) // LIST_ROWS]
@@ -47,86 +54,79 @@ def tile_picked_sidegate_sigmoid_l_kernel(tc, xT, side, w1_words, w1_scales, off
         nc.vector.memset(warm[:, 0:8], 0.0)
         nc.scalar.activation(out=warm[:, 8:16], in_=warm[:, 0:8], func=sigmoid)
 
-        x_rows = xT.rearrange("(g p u e) t -> g u p e t", g=2, p=P, u=2, e=2)
+        side_rows = [keep.tile([P, T], F32, name=f"side_rows{b}") for b in range(2)]
         raw = {}
 
-        def load_pair(pair):
-            for first, end, casts in PAIRS[pair]:
-                raw[pair, first] = keep.tile([P, 2, end - first], F32, name=f"raw{pair}_{first}", tag=f"raw{pair}_{first}", align_bytes=64)
+        first_pair = keep.tile([P, 2 * T], F32, name="first_pair", align_bytes=MX_ALIGN)
+        run = xT.rearrange("(g p u e) t -> g u p (e t)", g=2, p=P, u=2, e=2)[0, 0]
+        cut = T + PIECES[0][0][1]
+        nc.sync.dma_start(out=first_pair[:, 0:cut], in_=run[:, 0:cut])
+        nc.sync.dma_start(out=first_pair[:, cut : 2 * T], in_=run[:, cut : 2 * T])
+        for first, end, on_scalar in PIECES[0]:
+            raw[0, first] = first_pair[:].rearrange("p (e t) -> p e t", e=2)[:, :, first:end]
+
+        nc.sync.dma_start(offsets[:], offs)
+
+        x_rows = xT.rearrange("(g p u e) t -> g u p e t", g=2, p=P, u=2, e=2)
+        for pair in range(1, 4):
+            for first, end, on_scalar in PIECES[pair]:
+                raw[pair, first] = keep.tile([P, 2, end - first], F32, name=f"raw{pair}_{first}", align_bytes=MX_ALIGN)
                 nc.sync.dma_start(out=raw[pair, first][:], in_=x_rows[pair // 2, pair % 2, :, :, first:end])
 
-        def load_weights(queue):
-            for q in range(4):
-                queue.dma_start(
-                    out=w_scales[32 * q : 32 * q + 4, :, :].bitcast(I32),
-                    in_=w1_scales[:, 4 * q : 4 * q + 4, :].rearrange("g r n -> r g n").bitcast(I32),
-                )
-            queue.dma_start(out=w_codes[:].bitcast(I32), in_=w1_words.rearrange("g p n -> p g n").bitcast(I32))
-
-        side_rows = [keep.tile([P, T], F32, name=f"side_rows{b}") for b in range(2)]
-
-        def load_side(b):
+        for q in range(4):
+            nc.sync.dma_start(
+                out=w_scales[32 * q : 32 * q + 4, :, :].bitcast(I32),
+                in_=w1_scales[:, 4 * q : 4 * q + 4, :].rearrange("g r n -> r g n").bitcast(I32),
+            )
+        nc.sync.dma_start(out=w_codes[:].bitcast(I32), in_=w1_words.rearrange("g p n -> p g n").bitcast(I32))
+        for b in range(2):
             nc.sync.dma_start(out=side_rows[b][:], in_=side[b * P : (b + 1) * P, :])
 
-        load_pair(0)
-        nc.sync.dma_start(offsets[:], offs)
-        load_pair(1)
-        load_pair(2)
-        load_pair(3)
-        load_weights(nc.sync)
-        load_side(0)
-        load_side(1)
-
-        windows = {}
-        window_tags = {}
-
-        def cast(pair, which=None):
-            if pair not in windows:
-                windows[pair] = keep.tile([P, T, 2], BF16, name=f"window{pair}", tag=window_tags.get(pair, f"window{pair}"))
-            for n, (first, end, casts) in enumerate(PAIRS[pair]):
-                if which is not None and n != which:
-                    continue
-                lo = first
-                for hi, engine in casts:
-                    source = raw[pair, first][:, :, lo - first : hi - first].rearrange("p e (c i) -> p c e i", i=4)
-                    target = windows[pair][:, lo:hi, :].rearrange("p (c i) e -> p c e i", i=4)
-                    if engine == "v":
-                        nc.vector.tensor_copy(out=target, in_=source)
-                    else:
-                        nc.scalar.copy(out=target, in_=source)
-                    lo = hi
-
-        woven_first = keep.tile([P, S, 2], U32, name="woven0", tag="raw2_0", align_bytes=64)
+        windows = [keep.tile([P, T, 2], BF16, name=f"window{pair}") for pair in range(4)]
+        reused = {(0, 0): f"raw2_{PIECES[2][0][0]}", (0, 1): f"raw2_{PIECES[2][-1][0]}"}
         picked = {}
         woven = {}
         for g in range(2):
             for c in range(S // CHUNK[g]):
-                picked[g, c] = keep.tile([P, 2, CHUNK[g]], U32, name=f"picked{g}_{c}", tag=f"picked{g}_{c}")
-                if g == 0:
-                    woven[g, c] = woven_first[:, c * CHUNK[g] : (c + 1) * CHUNK[g], :]
-                else:
-                    woven[g, c] = keep.tile([P, CHUNK[g], 2], U32, name=f"woven{g}_{c}", align_bytes=64)[:]
-        code_tags = {(0, 1): "raw2_1280"}
-        x_codes = {
-            (g, h): keep.tile([P, BANK], U32, name=f"x_codes{g}_{h}", tag=code_tags.get((g, h), f"x_codes{g}_{h}"), align_bytes=64)
-            for g in range(2)
-            for h in range(2)
-        }
-        x_scales = {(g, h): keep.tile([P, BANK], U8, name=f"x_scales{g}_{h}", align_bytes=64) for g in range(2) for h in range(2)}
-        acc = {(b, h): psum.tile([P, BANK], F32, name=f"acc{b}_{h}") for b in range(2) for h in range(2)}
+                picked[g, c] = keep.tile([P, 2, CHUNK[g]], U32, name=f"picked{g}_{c}")
+                tag = reused.get((g, c), f"woven{g}_{c}")
+                woven[g, c] = keep.tile([P, CHUNK[g], 2], U32, name=f"woven{g}_{c}", tag=tag, align_bytes=MX_ALIGN)
+        halves = [(g, h) for g in range(2) for h in range(S // BANK)]
+        x_codes = {(g, h): keep.tile([P, BANK], U32, name=f"x_codes{g}_{h}", align_bytes=MX_ALIGN) for g, h in halves}
+        x_scales = {(g, h): keep.tile([P, BANK], U8, name=f"x_scales{g}_{h}", align_bytes=MX_ALIGN) for g, h in halves}
+        acc = {(b, first): psum.tile([P, BANK], F32, name=f"acc{b}_{first}") for b, first, count in GROUPS}
+        gates = keep.tile([P, 2 * S], F32, name="gates", tag="picked1_0")
 
-        def gather(pair, c):
+        def cast(pair, piece):
+            first, end, on_scalar = piece
+            split = end - on_scalar
+            for lo, hi, copy in [(first, split, nc.vector.tensor_copy), (split, end, nc.scalar.copy)]:
+                if lo < hi:
+                    copy(
+                        out=windows[pair][:, lo:hi, :].rearrange("p (c i) e -> p c e i", i=4),
+                        in_=raw[pair, first][:, :, lo - first : hi - first].rearrange("p e (c i) -> p c e i", i=4),
+                    )
+
+        def gather(pair):
             g, u = divmod(pair, 2)
             words = windows[pair][:].rearrange("p t e -> p (t e)").bitcast(U32)
-            nc.vector.tensor_copy(out=picked[g, c][:, u, :], in_=words.indirect(entries(c * CHUNK[g], CHUNK[g])))
+            for c in range(S // CHUNK[g]):
+                nc.vector.tensor_copy(out=picked[g, c][:, u, :], in_=words.indirect(entries(c * CHUNK[g], CHUNK[g])))
 
-        def weave(g, c, engine="s"):
-            target = woven[g, c].rearrange("p (j i) u -> p j u i", i=2)
-            source = picked[g, c][:].rearrange("p u (j i) -> p j u i", i=2)
-            if engine == "v":
-                nc.vector.tensor_copy(out=target.bitcast(I32), in_=source.bitcast(I32))
-            else:
+        def weave(g, c, on_scalar):
+            def views(lo, hi):
+                target = woven[g, c][:, lo:hi, :].rearrange("p (j i) u -> p j u i", i=2)
+                return target, picked[g, c][:, :, lo:hi].rearrange("p u (j i) -> p j u i", i=2)
+
+            if on_scalar > 0:
+                target, source = views(0, on_scalar)
                 nc.scalar.copy(out=target, in_=source)
+            if on_scalar < CHUNK[g]:
+                target, source = views(on_scalar, CHUNK[g])
+                nc.vector.tensor_copy(out=target.bitcast(I32), in_=source.bitcast(I32))
+
+        def weave_last_pass(c):
+            weave(1, c, min(max(SCALAR_WEAVES - c * CHUNK[1], 0), CHUNK[1]))
 
         def quantize(g, c):
             h, first = divmod(c * CHUNK[g], BANK)
@@ -134,75 +134,72 @@ def tile_picked_sidegate_sigmoid_l_kernel(tc, xT, side, w1_words, w1_scales, off
             nc.vector.quantize_mx(
                 out=x_codes[g, h][:, cols].bitcast(FP8X4),
                 scales=x_scales[g, h][:, cols],
-                in_=woven[g, c].rearrange("p j u -> p (j u)").bitcast(BF16),
+                in_=woven[g, c][:].rearrange("p j u -> p (j u)").bitcast(BF16),
             )
 
-        def multiply(g, b, h):
-            nc.tensor.matmul_mx(
-                out=acc[b, h][:],
-                lhsT=w_codes[:, g, 2 * P * b : 2 * P * (b + 1)].bitcast(FP4X4),
-                lhsT_scale=w_scales[:, g, P * b : P * (b + 1)],
-                rhs=x_codes[g, h][:].bitcast(FP8X4),
-                rhs_scale=x_scales[g, h][:],
-                start=(g == 0),
-                stop=(g == 1),
-            )
-
-        gates = keep.tile([P, 2 * S], F32, name="gates", tag="picked1_0")
+        def multiply(g, groups):
+            for b, first, count in groups:
+                h, inside = divmod(first, BANK)
+                nc.tensor.matmul_mx(
+                    out=acc[b, first][:, 0:count],
+                    lhsT=w_codes[:, g, 2 * P * b : 2 * P * (b + 1)].bitcast(FP4X4),
+                    lhsT_scale=w_scales[:, g, P * b : P * (b + 1)],
+                    rhs=x_codes[g, h][:, inside : inside + count].bitcast(FP8X4),
+                    rhs_scale=x_scales[g, h][:, inside : inside + count],
+                    start=(g == 0),
+                    stop=(g == 1),
+                )
 
         def gate(b, first, count):
             nc.scalar.activation(
-                out=gates[:, b * S + first : b * S + first + count], in_=side_rows[b][:].indirect(entries(first, count)), func=sigmoid
+                out=gates[:, b * S + first : b * S + first + count],
+                in_=side_rows[b][:].indirect(entries(first, count)),
+                func=sigmoid,
             )
 
-        def finish(b, first, count, queue=nc.sync, tag=None):
-            h, inside = divmod(first, BANK)
-            result = keep.tile([P, count], F32, name=f"result{b}_{first}", tag=tag or f"result{b}_{first}")
-            nc.vector.tensor_tensor(
-                out=result[:], in0=acc[b, h][:, inside : inside + count], in1=gates[:, b * S + first : b * S + first + count], op=mybir.AluOpType.mult
-            )
-            queue.dma_start(out=out[P * b : P * (b + 1), first : first + count], in_=result[:])
+        def finish(b, first, count):
+            result = keep.tile([P, count], F32, name=f"result{b}_{first}")
+            for block, start, width in GROUPS:
+                lo, hi = max(first, start), min(first + count, start + width)
+                if block == b and lo < hi:
+                    nc.vector.tensor_tensor(
+                        out=result[:, lo - first : hi - first],
+                        in0=acc[b, start][:, lo - start : hi - start],
+                        in1=gates[:, b * S + lo : b * S + hi],
+                        op=mybir.AluOpType.mult,
+                    )
+            nc.sync.dma_start(out=out[P * b : P * (b + 1), first : first + count], in_=result[:])
 
-        cast(0)
-        for c in range(2):
-            gather(0, c)
-        cast(1)
-        gather(1, 0)
-        gather(1, 1)
-        cast(2, 0)
-        weave(0, 0)
-        weave(0, 1)
-        cast(2, 1)
+        for pair in range(2):
+            for piece in PIECES[pair]:
+                cast(pair, piece)
+            gather(pair)
+        cast(2, PIECES[2][0])
+        weave(0, 0, CHUNK[0])
+        cast(2, PIECES[2][1])
         quantize(0, 0)
-        cast(2, 2)
-        for c in range(4):
-            gather(2, c)
+        cast(2, PIECES[2][2])
+        weave(0, 1, CHUNK[0])
+        gather(2)
         quantize(0, 1)
-        for h in range(2):
-            for b in range(2):
-                multiply(0, b, h)
-        cast(3)
-        for c in range(4):
-            gather(3, c)
-        weave(1, 0)
-        weave(1, 1, "v")
+        multiply(0, GROUPS)
+
+        for piece in PIECES[3]:
+            cast(3, piece)
+        gather(3)
+        weave_last_pass(0)
+        weave_last_pass(1)
         quantize(1, 0)
-        weave(1, 2, "v")
         quantize(1, 1)
-        multiply(1, 0, 0)
-        multiply(1, 1, 0)
-        weave(1, 3, "v")
+        multiply(1, WIDE_FIRST)
+        weave_last_pass(2)
+        weave_last_pass(3)
         quantize(1, 2)
+        multiply(1, NARROW[:2])
         quantize(1, 3)
-        multiply(1, 0, 1)
-        multiply(1, 1, 1)
-        gate(0, 0, 512)
-        gate(0, 512, 512)
-        gate(1, 0, 512)
-        gate(1, 512, 256)
-        gate(1, 768, 256)
-        finish(0, 0, 512)
-        finish(0, 512, 512)
-        finish(1, 0, 512)
-        finish(1, 512, 256)
-        finish(1, 768, 256)
+        multiply(1, NARROW[2:] + WIDE_LAST)
+
+        for piece in OUTPUTS:
+            gate(*piece)
+        for piece in OUTPUTS:
+            finish(*piece)

@@ -23,15 +23,12 @@ PIECES = [
     [(0, 1280, 480), (1280, T, 280)],
     [(0, 1408, 688), (1408, T, 240)],
     [(0, 512, 512), (512, 1280, 304), (1280, T, 304)],
-    [(0, 896, 896), (896, 1728, 416), (1728, T, 112)],
 ]
 CHUNK = [512, 256]
-SCALAR_WEAVES = 384
-WIDE_FIRST = [(0, 0, BANK), (1, 0, BANK)]
-NARROW = [(0, first, P) for first in range(BANK, S, P)]
-WIDE_LAST = [(1, BANK, BANK)]
-GROUPS = WIDE_FIRST + NARROW + WIDE_LAST
-OUTPUTS = [(0, 0, 512), (0, 512, 512), (1, 0, 512), (1, 512, 256), (1, 768, 256)]
+GROUPS = [(b, first, count) for b in range(2) for first, count in [(0, 512), (512, 256), (768, 256)]]
+CODE_TILES = [[(0, 512), (512, 512)], [(0, 512), (512, 256), (768, 256)]]
+OUTPUTS = [(0, 0, 512), (0, 512, 256), (0, 768, 256), (1, 0, 512), (1, 512, 256), (1, 768, 256)]
+HELPED = [(0, 768, 256), (1, 768, 256)]
 
 
 def tile_picked_sidegate_sigmoid_l_kernel(tc, xT, side, w1_words, w1_scales, offs, out):
@@ -68,10 +65,14 @@ def tile_picked_sidegate_sigmoid_l_kernel(tc, xT, side, w1_words, w1_scales, off
         nc.sync.dma_start(offsets[:], offs)
 
         x_rows = xT.rearrange("(g p u e) t -> g u p e t", g=2, p=P, u=2, e=2)
-        for pair in range(1, 4):
+        for pair in range(1, 3):
             for first, end, on_scalar in PIECES[pair]:
                 raw[pair, first] = keep.tile([P, 2, end - first], F32, name=f"raw{pair}_{first}", align_bytes=MX_ALIGN)
                 nc.sync.dma_start(out=raw[pair, first][:], in_=x_rows[pair // 2, pair % 2, :, :, first:end])
+
+        last_rows = [keep.tile([P, T], F32, name=f"last_row{e}") for e in range(2)]
+        for e in range(2):
+            nc.sync.dma_start(out=last_rows[e][:], in_=x_rows[1, 1, :, e, :])
 
         for q in range(4):
             nc.sync.dma_start(
@@ -82,20 +83,25 @@ def tile_picked_sidegate_sigmoid_l_kernel(tc, xT, side, w1_words, w1_scales, off
         for b in range(2):
             nc.sync.dma_start(out=side_rows[b][:], in_=side[b * P : (b + 1) * P, :])
 
-        windows = [keep.tile([P, T, 2], BF16, name=f"window{pair}") for pair in range(4)]
+        windows = [keep.tile([P, T, 2], BF16, name=f"window{pair}") for pair in range(3)]
         reused = {(0, 0): f"raw2_{PIECES[2][0][0]}", (0, 1): f"raw2_{PIECES[2][-1][0]}"}
         picked = {}
         woven = {}
         for g in range(2):
             for c in range(S // CHUNK[g]):
-                picked[g, c] = keep.tile([P, 2, CHUNK[g]], U32, name=f"picked{g}_{c}")
+                picked[g, c] = keep.tile([P, 2, CHUNK[g]], [U32, BF16][g], name=f"picked{g}_{c}")
                 tag = reused.get((g, c), f"woven{g}_{c}")
                 woven[g, c] = keep.tile([P, CHUNK[g], 2], U32, name=f"woven{g}_{c}", tag=tag, align_bytes=MX_ALIGN)
-        halves = [(g, h) for g in range(2) for h in range(S // BANK)]
-        x_codes = {(g, h): keep.tile([P, BANK], U32, name=f"x_codes{g}_{h}", align_bytes=MX_ALIGN) for g, h in halves}
-        x_scales = {(g, h): keep.tile([P, BANK], U8, name=f"x_scales{g}_{h}", align_bytes=MX_ALIGN) for g, h in halves}
+        parts = [(g, h, n) for g in range(2) for h, n in CODE_TILES[g]]
+        x_codes = {(g, h): keep.tile([P, n], U32, name=f"x_codes{g}_{h}", align_bytes=MX_ALIGN) for g, h, n in parts}
+        x_scales = {(g, h): keep.tile([P, n], U8, name=f"x_scales{g}_{h}", align_bytes=MX_ALIGN) for g, h, n in parts}
+
+        def code_tile(g, entry):
+            start = max(h for h, n in CODE_TILES[g] if h <= entry)
+            return start, entry - start
+
         acc = {(b, first): psum.tile([P, BANK], F32, name=f"acc{b}_{first}") for b, first, count in GROUPS}
-        gates = keep.tile([P, 2 * S], F32, name="gates", tag="picked1_0")
+        gates = {(b, first): keep.tile([P, count], F32, name=f"gates{b}_{first}") for b, first, count in OUTPUTS}
 
         def cast(pair, piece):
             first, end, on_scalar = piece
@@ -111,7 +117,20 @@ def tile_picked_sidegate_sigmoid_l_kernel(tc, xT, side, w1_words, w1_scales, off
             g, u = divmod(pair, 2)
             words = windows[pair][:].rearrange("p t e -> p (t e)").bitcast(U32)
             for c in range(S // CHUNK[g]):
-                nc.vector.tensor_copy(out=picked[g, c][:, u, :], in_=words.indirect(entries(c * CHUNK[g], CHUNK[g])))
+                target = picked[g, c][:, u, :] if g == 0 else woven[g, c][:, :, 0]
+                nc.vector.tensor_copy(out=target, in_=words.indirect(entries(c * CHUNK[g], CHUNK[g])))
+
+        def gather_row(e, on_vector):
+            for c in range(S // CHUNK[1]):
+                source = last_rows[e][:].indirect(entries(c * CHUNK[1], CHUNK[1]))
+                if c < on_vector:
+                    nc.vector.tensor_copy(out=picked[1, c][:, e, :], in_=source)
+                else:
+                    nc.scalar.activation(out=picked[1, c][:, e, :], in_=source, func=mybir.ActivationFunctionType.Copy)
+
+        def place(c):
+            values = woven[1, c][:].rearrange("p j u -> p (j u)").bitcast(BF16).rearrange("p (j t) -> p j t", t=4)
+            nc.vector.tensor_copy(out=values[:, :, 2:4], in_=picked[1, c][:].rearrange("p e j -> p j e"))
 
         def weave(g, c, on_scalar):
             def views(lo, hi):
@@ -125,11 +144,8 @@ def tile_picked_sidegate_sigmoid_l_kernel(tc, xT, side, w1_words, w1_scales, off
                 target, source = views(on_scalar, CHUNK[g])
                 nc.vector.tensor_copy(out=target.bitcast(I32), in_=source.bitcast(I32))
 
-        def weave_last_pass(c):
-            weave(1, c, min(max(SCALAR_WEAVES - c * CHUNK[1], 0), CHUNK[1]))
-
         def quantize(g, c):
-            h, first = divmod(c * CHUNK[g], BANK)
+            h, first = code_tile(g, c * CHUNK[g])
             cols = slice(first, first + CHUNK[g])
             nc.vector.quantize_mx(
                 out=x_codes[g, h][:, cols].bitcast(FP8X4),
@@ -139,7 +155,7 @@ def tile_picked_sidegate_sigmoid_l_kernel(tc, xT, side, w1_words, w1_scales, off
 
         def multiply(g, groups):
             for b, first, count in groups:
-                h, inside = divmod(first, BANK)
+                h, inside = code_tile(g, first)
                 nc.tensor.matmul_mx(
                     out=acc[b, first][:, 0:count],
                     lhsT=w_codes[:, g, 2 * P * b : 2 * P * (b + 1)].bitcast(FP4X4),
@@ -151,11 +167,12 @@ def tile_picked_sidegate_sigmoid_l_kernel(tc, xT, side, w1_words, w1_scales, off
                 )
 
         def gate(b, first, count):
-            nc.scalar.activation(
-                out=gates[:, b * S + first : b * S + first + count],
-                in_=side_rows[b][:].indirect(entries(first, count)),
-                func=sigmoid,
-            )
+            source = side_rows[b][:].indirect(entries(first, count))
+            if (b, first, count) in HELPED:
+                fetched = keep.tile([P, count], F32, name=f"fetched{b}_{first}")
+                nc.vector.tensor_copy(out=fetched[:], in_=source)
+                source = fetched[:]
+            nc.scalar.activation(out=gates[b, first][:], in_=source, func=sigmoid)
 
         def finish(b, first, count):
             result = keep.tile([P, count], F32, name=f"result{b}_{first}")
@@ -165,7 +182,7 @@ def tile_picked_sidegate_sigmoid_l_kernel(tc, xT, side, w1_words, w1_scales, off
                     nc.vector.tensor_tensor(
                         out=result[:, lo - first : hi - first],
                         in0=acc[b, start][:, lo - start : hi - start],
-                        in1=gates[:, b * S + lo : b * S + hi],
+                        in1=gates[b, first][:, lo - first : hi - first],
                         op=mybir.AluOpType.mult,
                     )
             nc.sync.dma_start(out=out[P * b : P * (b + 1), first : first + count], in_=result[:])
@@ -184,20 +201,17 @@ def tile_picked_sidegate_sigmoid_l_kernel(tc, xT, side, w1_words, w1_scales, off
         quantize(0, 1)
         multiply(0, GROUPS)
 
-        for piece in PIECES[3]:
-            cast(3, piece)
-        gather(3)
-        weave_last_pass(0)
-        weave_last_pass(1)
+        gather_row(0, 0)
+        gather_row(1, 1)
+        place(0)
+        place(1)
         quantize(1, 0)
         quantize(1, 1)
-        multiply(1, WIDE_FIRST)
-        weave_last_pass(2)
-        weave_last_pass(3)
+        place(2)
+        place(3)
         quantize(1, 2)
-        multiply(1, NARROW[:2])
         quantize(1, 3)
-        multiply(1, NARROW[2:] + WIDE_LAST)
+        multiply(1, GROUPS)
 
         for piece in OUTPUTS:
             gate(*piece)

@@ -25,10 +25,10 @@ PIECES = [
     [(0, 512, 512), (512, 1280, 304), (1280, T, 304)],
 ]
 CHUNK = [512, 256]
-GROUPS = [(b, first, count) for b in range(2) for first, count in [(0, 512), (512, 256), (768, 256)]]
-CODE_TILES = [[(0, 512), (512, 512)], [(0, 512), (512, 256), (768, 256)]]
-OUTPUTS = [(0, 0, 512), (0, 512, 256), (0, 768, 256), (1, 0, 512), (1, 512, 256), (1, 768, 256)]
-HELPED = [(0, 768, 256), (1, 768, 256)]
+GROUPS = [(b, first, count) for b in range(2) for first, count in [(0, 512), (512, 512)]]
+CODE_TILES = [[(0, 512), (512, 512)], [(0, 512), (512, 512)]]
+OUTPUTS = [(0, 0, 512), (0, 512, 512), (1, 0, 512), (1, 512, 256), (1, 768, 256)]
+HELPED = [(1, 768, 256)]
 
 
 def tile_picked_sidegate_sigmoid_l_kernel(tc, xT, side, w1_words, w1_scales, offs, out):
@@ -45,7 +45,18 @@ def tile_picked_sidegate_sigmoid_l_kernel(tc, xT, side, w1_words, w1_scales, off
         def entries(first, count):
             return offsets[:, first // LIST_ROWS : (first + count) // LIST_ROWS]
 
-        nc.vector.memset(w_scales[:].rearrange("p g n -> p (g n)").bitcast(I32), 0)
+        nc.gpsimd.memset(w_scales[:].rearrange("p g n -> p (g n)").bitcast(I32), 0)
+
+        scale_rows = keep.tile([P, 2, N], U8, name="scale_rows")
+        for q in range(4):
+            nc.scalar.dma_start(
+                out=scale_rows[32 * q : 32 * q + 4, :, :].bitcast(I32),
+                in_=w1_scales[:, 4 * q : 4 * q + 4, :].rearrange("g r n -> r g n").bitcast(I32),
+            )
+            nc.gpsimd.tensor_copy(
+                out=w_scales[32 * q : 32 * q + 4, :, :].bitcast(I32),
+                in_=scale_rows[32 * q : 32 * q + 4, :, :].bitcast(I32),
+            )
 
         warm = keep.tile([P, 16], F32, name="warm")
         nc.vector.memset(warm[:, 0:8], 0.0)
@@ -74,11 +85,6 @@ def tile_picked_sidegate_sigmoid_l_kernel(tc, xT, side, w1_words, w1_scales, off
         for e in range(2):
             nc.sync.dma_start(out=last_rows[e][:], in_=x_rows[1, 1, :, e, :])
 
-        for q in range(4):
-            nc.sync.dma_start(
-                out=w_scales[32 * q : 32 * q + 4, :, :].bitcast(I32),
-                in_=w1_scales[:, 4 * q : 4 * q + 4, :].rearrange("g r n -> r g n").bitcast(I32),
-            )
         nc.sync.dma_start(out=w_codes[:].bitcast(I32), in_=w1_words.rearrange("g p n -> p g n").bitcast(I32))
         for b in range(2):
             nc.sync.dma_start(out=side_rows[b][:], in_=side[b * P : (b + 1) * P, :])

@@ -19,14 +19,11 @@ BANK = 512
 LIST_ROWS = 16
 MX_ALIGN = 64
 
-PIECES = [
-    [(0, 1280, 480), (1280, T, 280)],
-    [(0, 1408, 688), (1408, T, 240)],
-    [(0, 512, 512), (512, 1280, 304), (1280, T, 304)],
-]
-CHUNK = [512, 256]
-GROUPS = [(b, first, count) for b in range(2) for first, count in [(0, 512), (512, 512)]]
-CODE_TILES = [[(0, 512), (512, 512)], [(0, 512), (512, 512)]]
+PIECES = [[(0, 1280, 432), (1280, T, 256)], [(0, 1024, 960), (1024, 1536, 0), (1536, T, 168)]]
+CHUNK = 256
+PARTS = [[(0, 512), (512, 512)], [(0, 256), (256, 256), (512, 256), (768, 256)]]
+ON_VECTOR = [(0, 1, 0), (1, 1, 0)]
+GROUPS = [(b, first, BANK) for b in range(2) for first in range(0, S, BANK)]
 OUTPUTS = [(0, 0, 512), (0, 512, 512), (1, 0, 512), (1, 512, 256), (1, 768, 256)]
 HELPED = [(1, 768, 256)]
 
@@ -41,22 +38,19 @@ def tile_picked_sidegate_sigmoid_l_kernel(tc, xT, side, w1_words, w1_scales, off
         offsets = keep.tile([P, S // LIST_ROWS], U16, name="offsets")
         w_codes = keep.tile([P, 2, 2 * N], U8, name="w_codes", align_bytes=MX_ALIGN)
         w_scales = keep.tile([P, 2, N], U8, name="w_scales", align_bytes=MX_ALIGN)
+        scale_rows = keep.tile([P, 2, N], U8, name="scale_rows")
 
         def entries(first, count):
             return offsets[:, first // LIST_ROWS : (first + count) // LIST_ROWS]
 
         nc.gpsimd.memset(w_scales[:].rearrange("p g n -> p (g n)").bitcast(I32), 0)
-
-        scale_rows = keep.tile([P, 2, N], U8, name="scale_rows")
         for q in range(4):
+            rows = slice(32 * q, 32 * q + 4)
             nc.scalar.dma_start(
-                out=scale_rows[32 * q : 32 * q + 4, :, :].bitcast(I32),
+                out=scale_rows[rows, :, :].bitcast(I32),
                 in_=w1_scales[:, 4 * q : 4 * q + 4, :].rearrange("g r n -> r g n").bitcast(I32),
             )
-            nc.gpsimd.tensor_copy(
-                out=w_scales[32 * q : 32 * q + 4, :, :].bitcast(I32),
-                in_=scale_rows[32 * q : 32 * q + 4, :, :].bitcast(I32),
-            )
+            nc.gpsimd.tensor_copy(out=w_scales[rows, :, :].bitcast(I32), in_=scale_rows[rows, :, :].bitcast(I32))
 
         warm = keep.tile([P, 16], F32, name="warm")
         nc.vector.memset(warm[:, 0:8], 0.0)
@@ -64,7 +58,6 @@ def tile_picked_sidegate_sigmoid_l_kernel(tc, xT, side, w1_words, w1_scales, off
 
         side_rows = [keep.tile([P, T], F32, name=f"side_rows{b}") for b in range(2)]
         raw = {}
-
         first_pair = keep.tile([P, 2 * T], F32, name="first_pair", align_bytes=MX_ALIGN)
         run = xT.rearrange("(g p u e) t -> g u p (e t)", g=2, p=P, u=2, e=2)[0, 0]
         cut = T + PIECES[0][0][1]
@@ -72,102 +65,81 @@ def tile_picked_sidegate_sigmoid_l_kernel(tc, xT, side, w1_words, w1_scales, off
         nc.sync.dma_start(out=first_pair[:, cut : 2 * T], in_=run[:, cut : 2 * T])
         for first, end, on_scalar in PIECES[0]:
             raw[0, first] = first_pair[:].rearrange("p (e t) -> p e t", e=2)[:, :, first:end]
-
         nc.sync.dma_start(offsets[:], offs)
 
         x_rows = xT.rearrange("(g p u e) t -> g u p e t", g=2, p=P, u=2, e=2)
-        for pair in range(1, 3):
-            for first, end, on_scalar in PIECES[pair]:
-                raw[pair, first] = keep.tile([P, 2, end - first], F32, name=f"raw{pair}_{first}", align_bytes=MX_ALIGN)
-                nc.sync.dma_start(out=raw[pair, first][:], in_=x_rows[pair // 2, pair % 2, :, :, first:end])
-
-        last_rows = [keep.tile([P, T], F32, name=f"last_row{e}") for e in range(2)]
+        single = {(g, e): keep.tile([P, T], F32, name=f"single{g}_{e}") for g in range(2) for e in range(2)}
         for e in range(2):
-            nc.sync.dma_start(out=last_rows[e][:], in_=x_rows[1, 1, :, e, :])
-
+            nc.sync.dma_start(out=single[0, e][:], in_=x_rows[0, 1, :, e, :])
+        for first, end, on_scalar in PIECES[1]:
+            raw[1, first] = keep.tile([P, 2, end - first], F32, name=f"raw1_{first}", align_bytes=MX_ALIGN)
+            nc.sync.dma_start(out=raw[1, first][:], in_=x_rows[1, 0, :, :, first:end])
+        for e in range(2):
+            nc.sync.dma_start(out=single[1, e][:], in_=x_rows[1, 1, :, e, :])
         nc.sync.dma_start(out=w_codes[:].bitcast(I32), in_=w1_words.rearrange("g p n -> p g n").bitcast(I32))
         for b in range(2):
             nc.sync.dma_start(out=side_rows[b][:], in_=side[b * P : (b + 1) * P, :])
 
-        windows = [keep.tile([P, T, 2], BF16, name=f"window{pair}") for pair in range(3)]
-        reused = {(0, 0): f"raw2_{PIECES[2][0][0]}", (0, 1): f"raw2_{PIECES[2][-1][0]}"}
-        picked = {}
-        woven = {}
-        for g in range(2):
-            for c in range(S // CHUNK[g]):
-                picked[g, c] = keep.tile([P, 2, CHUNK[g]], [U32, BF16][g], name=f"picked{g}_{c}")
-                tag = reused.get((g, c), f"woven{g}_{c}")
-                woven[g, c] = keep.tile([P, CHUNK[g], 2], U32, name=f"woven{g}_{c}", tag=tag, align_bytes=MX_ALIGN)
-        parts = [(g, h, n) for g in range(2) for h, n in CODE_TILES[g]]
-        x_codes = {(g, h): keep.tile([P, n], U32, name=f"x_codes{g}_{h}", align_bytes=MX_ALIGN) for g, h, n in parts}
-        x_scales = {(g, h): keep.tile([P, n], U8, name=f"x_scales{g}_{h}", align_bytes=MX_ALIGN) for g, h, n in parts}
-
-        def code_tile(g, entry):
-            start = max(h for h, n in CODE_TILES[g] if h <= entry)
-            return start, entry - start
-
+        windows = [keep.tile([P, T, 2], BF16, name=f"window{g}") for g in range(2)]
+        planes = {(g, c): keep.tile([P, 2, CHUNK], BF16, name=f"planes{g}_{c}") for g in range(2) for c in range(S // CHUNK)}
+        woven = {
+            (g, first): keep.tile([P, count, 2], U32, name=f"woven{g}_{first}", align_bytes=MX_ALIGN)
+            for g in range(2)
+            for first, count in PARTS[g]
+        }
+        halves = [(g, h) for g in range(2) for h in range(S // BANK)]
+        x_codes = {(g, h): keep.tile([P, BANK], U32, name=f"x_codes{g}_{h}", align_bytes=MX_ALIGN) for g, h in halves}
+        x_scales = {(g, h): keep.tile([P, BANK], U8, name=f"x_scales{g}_{h}", align_bytes=MX_ALIGN) for g, h in halves}
         acc = {(b, first): psum.tile([P, BANK], F32, name=f"acc{b}_{first}") for b, first, count in GROUPS}
         gates = {(b, first): keep.tile([P, count], F32, name=f"gates{b}_{first}") for b, first, count in OUTPUTS}
 
-        def cast(pair, piece):
+        def cast(g, piece):
             first, end, on_scalar = piece
             split = end - on_scalar
             for lo, hi, copy in [(first, split, nc.vector.tensor_copy), (split, end, nc.scalar.copy)]:
                 if lo < hi:
                     copy(
-                        out=windows[pair][:, lo:hi, :].rearrange("p (c i) e -> p c e i", i=4),
-                        in_=raw[pair, first][:, :, lo - first : hi - first].rearrange("p e (c i) -> p c e i", i=4),
+                        out=windows[g][:, lo:hi, :].rearrange("p (c i) e -> p c e i", i=4),
+                        in_=raw[g, first][:, :, lo - first : hi - first].rearrange("p e (c i) -> p c e i", i=4),
                     )
 
-        def gather(pair):
-            g, u = divmod(pair, 2)
-            words = windows[pair][:].rearrange("p t e -> p (t e)").bitcast(U32)
-            for c in range(S // CHUNK[g]):
-                target = picked[g, c][:, u, :] if g == 0 else woven[g, c][:, :, 0]
-                nc.vector.tensor_copy(out=target, in_=words.indirect(entries(c * CHUNK[g], CHUNK[g])))
+        def gather_pair(g):
+            words = windows[g][:].rearrange("p t e -> p (t e)").bitcast(U32)
+            for first, count in PARTS[g]:
+                nc.vector.tensor_copy(out=woven[g, first][:, :, 0], in_=words.indirect(entries(first, count)))
 
-        def gather_row(e, on_vector):
-            for c in range(S // CHUNK[1]):
-                source = last_rows[e][:].indirect(entries(c * CHUNK[1], CHUNK[1]))
-                if c < on_vector:
-                    nc.vector.tensor_copy(out=picked[1, c][:, e, :], in_=source)
+        def gather_row(g, e):
+            for c in range(S // CHUNK):
+                source = single[g, e][:].indirect(entries(c * CHUNK, CHUNK))
+                if (g, e, c) in ON_VECTOR:
+                    nc.vector.tensor_copy(out=planes[g, c][:, e, :], in_=source)
                 else:
-                    nc.scalar.activation(out=picked[1, c][:, e, :], in_=source, func=mybir.ActivationFunctionType.Copy)
+                    nc.scalar.activation(out=planes[g, c][:, e, :], in_=source, func=mybir.ActivationFunctionType.Copy)
 
-        def place(c):
-            values = woven[1, c][:].rearrange("p j u -> p (j u)").bitcast(BF16).rearrange("p (j t) -> p j t", t=4)
-            nc.vector.tensor_copy(out=values[:, :, 2:4], in_=picked[1, c][:].rearrange("p e j -> p j e"))
+        def place(g, c):
+            start = max(first for first, count in PARTS[g] if first <= c * CHUNK)
+            inside = c * CHUNK - start
+            values = woven[g, start][:].rearrange("p j u -> p (j u)").bitcast(BF16).rearrange("p (j t) -> p j t", t=4)
+            nc.vector.tensor_copy(out=values[:, inside : inside + CHUNK, 2:4], in_=planes[g, c][:].rearrange("p e j -> p j e"))
 
-        def weave(g, c, on_scalar):
-            def views(lo, hi):
-                target = woven[g, c][:, lo:hi, :].rearrange("p (j i) u -> p j u i", i=2)
-                return target, picked[g, c][:, :, lo:hi].rearrange("p u (j i) -> p j u i", i=2)
-
-            if on_scalar > 0:
-                target, source = views(0, on_scalar)
-                nc.scalar.copy(out=target, in_=source)
-            if on_scalar < CHUNK[g]:
-                target, source = views(on_scalar, CHUNK[g])
-                nc.vector.tensor_copy(out=target.bitcast(I32), in_=source.bitcast(I32))
-
-        def quantize(g, c):
-            h, first = code_tile(g, c * CHUNK[g])
-            cols = slice(first, first + CHUNK[g])
+        def quantize(g, part):
+            first, count = part
+            h, inside = divmod(first, BANK)
             nc.vector.quantize_mx(
-                out=x_codes[g, h][:, cols].bitcast(FP8X4),
-                scales=x_scales[g, h][:, cols],
-                in_=woven[g, c][:].rearrange("p j u -> p (j u)").bitcast(BF16),
+                out=x_codes[g, h][:, inside : inside + count].bitcast(FP8X4),
+                scales=x_scales[g, h][:, inside : inside + count],
+                in_=woven[g, first][:].rearrange("p j u -> p (j u)").bitcast(BF16),
             )
 
-        def multiply(g, groups):
-            for b, first, count in groups:
-                h, inside = code_tile(g, first)
+        def multiply(g):
+            for b, first, count in GROUPS:
+                h = first // BANK
                 nc.tensor.matmul_mx(
-                    out=acc[b, first][:, 0:count],
+                    out=acc[b, first][:],
                     lhsT=w_codes[:, g, 2 * P * b : 2 * P * (b + 1)].bitcast(FP4X4),
                     lhsT_scale=w_scales[:, g, P * b : P * (b + 1)],
-                    rhs=x_codes[g, h][:, inside : inside + count].bitcast(FP8X4),
-                    rhs_scale=x_scales[g, h][:, inside : inside + count],
+                    rhs=x_codes[g, h][:].bitcast(FP8X4),
+                    rhs_scale=x_scales[g, h][:],
                     start=(g == 0),
                     stop=(g == 1),
                 )
@@ -182,42 +154,29 @@ def tile_picked_sidegate_sigmoid_l_kernel(tc, xT, side, w1_words, w1_scales, off
 
         def finish(b, first, count):
             result = keep.tile([P, count], F32, name=f"result{b}_{first}")
-            for block, start, width in GROUPS:
-                lo, hi = max(first, start), min(first + count, start + width)
-                if block == b and lo < hi:
-                    nc.vector.tensor_tensor(
-                        out=result[:, lo - first : hi - first],
-                        in0=acc[b, start][:, lo - start : hi - start],
-                        in1=gates[b, first][:, lo - first : hi - first],
-                        op=mybir.AluOpType.mult,
-                    )
+            start = first // BANK * BANK
+            nc.vector.tensor_tensor(
+                out=result[:],
+                in0=acc[b, start][:, first - start : first - start + count],
+                in1=gates[b, first][:],
+                op=mybir.AluOpType.mult,
+            )
             nc.sync.dma_start(out=out[P * b : P * (b + 1), first : first + count], in_=result[:])
 
-        for pair in range(2):
-            for piece in PIECES[pair]:
-                cast(pair, piece)
-            gather(pair)
-        cast(2, PIECES[2][0])
-        weave(0, 0, CHUNK[0])
-        cast(2, PIECES[2][1])
-        quantize(0, 0)
-        cast(2, PIECES[2][2])
-        weave(0, 1, CHUNK[0])
-        gather(2)
-        quantize(0, 1)
-        multiply(0, GROUPS)
-
-        gather_row(0, 0)
-        gather_row(1, 1)
-        place(0)
-        place(1)
-        quantize(1, 0)
-        quantize(1, 1)
-        place(2)
-        place(3)
-        quantize(1, 2)
-        quantize(1, 3)
-        multiply(1, GROUPS)
+        for g in range(2):
+            for piece in PIECES[g]:
+                cast(g, piece)
+            gather_pair(g)
+            gather_row(g, 0)
+            gather_row(g, 1)
+            placed = 0
+            for first, count in PARTS[g]:
+                ahead = min((first + count) // CHUNK + 1, S // CHUNK)
+                for c in range(placed, ahead):
+                    place(g, c)
+                placed = ahead
+                quantize(g, (first, count))
+            multiply(g)
 
         for piece in OUTPUTS:
             gate(*piece)

@@ -19,10 +19,11 @@ BANK = 512
 LIST_ROWS = 16
 MX_ALIGN = 64
 
-PIECES = [[(0, 1280, 432), (1280, T, 256)], [(0, 1024, 960), (1024, 1536, 0), (1536, T, 168)]]
-CHUNK = 256
-PARTS = [[(0, 512), (512, 512)], [(0, 256), (256, 256), (512, 256), (768, 256)]]
-ON_VECTOR = [(0, 1, 0), (1, 1, 0)]
+COARSE = [(0, 256), (256, 256), (512, 512)]
+FINE = [(first, 256) for first in range(0, S, 256)]
+STEPS = {(0, 0): COARSE, (0, 1): COARSE, (1, 0): COARSE, (1, 1): FINE}
+PARTS = [[(0, 512), (512, 512)], FINE]
+ON_VECTOR = {(0, 0): 2, (0, 1): 2, (0, 2): 0}
 GROUPS = [(b, first, BANK) for b in range(2) for first in range(0, S, BANK)]
 OUTPUTS = [(0, 0, 512), (0, 512, 512), (1, 0, 512), (1, 512, 256), (1, 768, 256)]
 HELPED = [(1, 768, 256)]
@@ -45,90 +46,71 @@ def tile_picked_sidegate_sigmoid_l_kernel(tc, xT, side, w1_words, w1_scales, off
 
         nc.gpsimd.memset(w_scales[:].rearrange("p g n -> p (g n)").bitcast(I32), 0)
         for q in range(4):
-            rows = slice(32 * q, 32 * q + 4)
+            live = slice(32 * q, 32 * q + 4)
             nc.scalar.dma_start(
-                out=scale_rows[rows, :, :].bitcast(I32),
+                out=scale_rows[live, :, :].bitcast(I32),
                 in_=w1_scales[:, 4 * q : 4 * q + 4, :].rearrange("g r n -> r g n").bitcast(I32),
             )
-            nc.gpsimd.tensor_copy(out=w_scales[rows, :, :].bitcast(I32), in_=scale_rows[rows, :, :].bitcast(I32))
+            nc.gpsimd.tensor_copy(out=w_scales[live, :, :].bitcast(I32), in_=scale_rows[live, :, :].bitcast(I32))
 
         warm = keep.tile([P, 16], F32, name="warm")
         nc.vector.memset(warm[:, 0:8], 0.0)
         nc.scalar.activation(out=warm[:, 8:16], in_=warm[:, 0:8], func=sigmoid)
 
         side_rows = [keep.tile([P, T], F32, name=f"side_rows{b}") for b in range(2)]
-        raw = {}
-        first_pair = keep.tile([P, 2 * T], F32, name="first_pair", align_bytes=MX_ALIGN)
-        run = xT.rearrange("(g p u e) t -> g u p (e t)", g=2, p=P, u=2, e=2)[0, 0]
-        cut = T + PIECES[0][0][1]
-        nc.sync.dma_start(out=first_pair[:, 0:cut], in_=run[:, 0:cut])
-        nc.sync.dma_start(out=first_pair[:, cut : 2 * T], in_=run[:, cut : 2 * T])
-        for first, end, on_scalar in PIECES[0]:
-            raw[0, first] = first_pair[:].rearrange("p (e t) -> p e t", e=2)[:, :, first:end]
+        x_rows = xT.rearrange("(g p t) c -> g p t c", g=2, p=P, t=4)
+        first_rows = keep.tile([P, 2, T], F32, name="first_rows")
+        nc.sync.dma_start(out=first_rows[:], in_=x_rows[0, :, 0:2, :])
         nc.sync.dma_start(offsets[:], offs)
-
-        x_rows = xT.rearrange("(g p u e) t -> g u p e t", g=2, p=P, u=2, e=2)
-        single = {(g, e): keep.tile([P, T], F32, name=f"single{g}_{e}") for g in range(2) for e in range(2)}
-        for e in range(2):
-            nc.sync.dma_start(out=single[0, e][:], in_=x_rows[0, 1, :, e, :])
-        for first, end, on_scalar in PIECES[1]:
-            raw[1, first] = keep.tile([P, 2, end - first], F32, name=f"raw1_{first}", align_bytes=MX_ALIGN)
-            nc.sync.dma_start(out=raw[1, first][:], in_=x_rows[1, 0, :, :, first:end])
-        for e in range(2):
-            nc.sync.dma_start(out=single[1, e][:], in_=x_rows[1, 1, :, e, :])
+        rows = {(0, t): first_rows[:, t, :] for t in range(2)}
+        for g, t in [(g, t) for g in range(2) for t in range(4)][2:]:
+            rows[g, t] = keep.tile([P, T], F32, name=f"row{g}_{t}")[:]
+            nc.sync.dma_start(out=rows[g, t], in_=x_rows[g, :, t, :])
         nc.sync.dma_start(out=w_codes[:].bitcast(I32), in_=w1_words.rearrange("g p n -> p g n").bitcast(I32))
-        for b in range(2):
-            nc.sync.dma_start(out=side_rows[b][:], in_=side[b * P : (b + 1) * P, :])
+        nc.sync.dma_start(out=side_rows[0][:], in_=side[0:P, :])
+        nc.sync.dma_start(out=side_rows[1][:], in_=side[P : 2 * P, :])
 
-        windows = [keep.tile([P, T, 2], BF16, name=f"window{g}") for g in range(2)]
-        planes = {(g, c): keep.tile([P, 2, CHUNK], BF16, name=f"planes{g}_{c}") for g in range(2) for c in range(S // CHUNK)}
+        planes = {
+            (g, u, first): keep.tile([P, 2, count], F32 if (g, u) == (0, 0) else BF16, name=f"planes{g}_{u}_{first}")
+            for g in range(2)
+            for u in range(2)
+            for first, count in STEPS[g, u]
+        }
+        halves = [(g, h) for g in range(2) for h in range(S // BANK)]
         woven = {
-            (g, first): keep.tile([P, count, 2], U32, name=f"woven{g}_{first}", align_bytes=MX_ALIGN)
+            (g, first): keep.tile([P, count, 4], BF16, name=f"woven{g}_{first}", align_bytes=MX_ALIGN)
             for g in range(2)
             for first, count in PARTS[g]
         }
-        halves = [(g, h) for g in range(2) for h in range(S // BANK)]
         x_codes = {(g, h): keep.tile([P, BANK], U32, name=f"x_codes{g}_{h}", align_bytes=MX_ALIGN) for g, h in halves}
         x_scales = {(g, h): keep.tile([P, BANK], U8, name=f"x_scales{g}_{h}", align_bytes=MX_ALIGN) for g, h in halves}
         acc = {(b, first): psum.tile([P, BANK], F32, name=f"acc{b}_{first}") for b, first, count in GROUPS}
         gates = {(b, first): keep.tile([P, count], F32, name=f"gates{b}_{first}") for b, first, count in OUTPUTS}
 
-        def cast(g, piece):
-            first, end, on_scalar = piece
-            split = end - on_scalar
-            for lo, hi, copy in [(first, split, nc.vector.tensor_copy), (split, end, nc.scalar.copy)]:
+        def gather_row(g, t):
+            u, e = divmod(t, 2)
+            for step, (first, count) in enumerate(STEPS[g, u]):
+                source = rows[g, t].indirect(entries(first, count))
+                if step < ON_VECTOR.get((g, t), 1):
+                    nc.vector.tensor_copy(out=planes[g, u, first][:, e, :], in_=source)
+                else:
+                    nc.scalar.activation(out=planes[g, u, first][:, e, :], in_=source, func=mybir.ActivationFunctionType.Copy)
+
+        def place(g, u, first, count):
+            for start, width in PARTS[g]:
+                lo, hi = max(first, start), min(first + count, start + width)
                 if lo < hi:
-                    copy(
-                        out=windows[g][:, lo:hi, :].rearrange("p (c i) e -> p c e i", i=4),
-                        in_=raw[g, first][:, :, lo - first : hi - first].rearrange("p e (c i) -> p c e i", i=4),
+                    nc.vector.tensor_copy(
+                        out=woven[g, start][:, lo - start : hi - start, 2 * u : 2 * u + 2],
+                        in_=planes[g, u, first][:, :, lo - first : hi - first].rearrange("p e j -> p j e"),
                     )
 
-        def gather_pair(g):
-            words = windows[g][:].rearrange("p t e -> p (t e)").bitcast(U32)
-            for first, count in PARTS[g]:
-                nc.vector.tensor_copy(out=woven[g, first][:, :, 0], in_=words.indirect(entries(first, count)))
-
-        def gather_row(g, e):
-            for c in range(S // CHUNK):
-                source = single[g, e][:].indirect(entries(c * CHUNK, CHUNK))
-                if (g, e, c) in ON_VECTOR:
-                    nc.vector.tensor_copy(out=planes[g, c][:, e, :], in_=source)
-                else:
-                    nc.scalar.activation(out=planes[g, c][:, e, :], in_=source, func=mybir.ActivationFunctionType.Copy)
-
-        def place(g, c):
-            start = max(first for first, count in PARTS[g] if first <= c * CHUNK)
-            inside = c * CHUNK - start
-            values = woven[g, start][:].rearrange("p j u -> p (j u)").bitcast(BF16).rearrange("p (j t) -> p j t", t=4)
-            nc.vector.tensor_copy(out=values[:, inside : inside + CHUNK, 2:4], in_=planes[g, c][:].rearrange("p e j -> p j e"))
-
-        def quantize(g, part):
-            first, count = part
+        def quantize(g, first, count):
             h, inside = divmod(first, BANK)
             nc.vector.quantize_mx(
                 out=x_codes[g, h][:, inside : inside + count].bitcast(FP8X4),
                 scales=x_scales[g, h][:, inside : inside + count],
-                in_=woven[g, first][:].rearrange("p j u -> p (j u)").bitcast(BF16),
+                in_=woven[g, first][:].rearrange("p j t -> p (j t)"),
             )
 
         def multiply(g):
@@ -164,18 +146,19 @@ def tile_picked_sidegate_sigmoid_l_kernel(tc, xT, side, w1_words, w1_scales, off
             nc.sync.dma_start(out=out[P * b : P * (b + 1), first : first + count], in_=result[:])
 
         for g in range(2):
-            for piece in PIECES[g]:
-                cast(g, piece)
-            gather_pair(g)
             gather_row(g, 0)
             gather_row(g, 1)
+            for step in STEPS[g, 0]:
+                place(g, 0, *step)
+            gather_row(g, 2)
+            gather_row(g, 3)
             placed = 0
             for first, count in PARTS[g]:
-                ahead = min((first + count) // CHUNK + 1, S // CHUNK)
-                for c in range(placed, ahead):
-                    place(g, c)
-                placed = ahead
-                quantize(g, (first, count))
+                for step in STEPS[g, 1]:
+                    if placed <= step[0] <= first + count:
+                        place(g, 1, *step)
+                placed = first + count + 1
+                quantize(g, first, count)
             multiply(g)
 
         for piece in OUTPUTS:

@@ -18,15 +18,16 @@ P = 128
 BANK = 512
 LIST_ROWS = 16
 MX_ALIGN = 64
+QUARTER = S // 4
 
-COARSE = [(0, 256), (256, 256), (512, 512)]
-FINE = [(first, 256) for first in range(0, S, 256)]
-STEPS = {(0, 0): COARSE, (0, 1): COARSE, (1, 0): COARSE, (1, 1): FINE}
-PARTS = [[(0, 512), (512, 512)], FINE]
-ON_VECTOR = {(0, 0): 2, (0, 1): 2, (0, 2): 0}
-GROUPS = [(b, first, BANK) for b in range(2) for first in range(0, S, BANK)]
-OUTPUTS = [(0, 0, 512), (0, 512, 512), (1, 0, 512), (1, 512, 256), (1, 768, 256)]
-HELPED = [(1, 768, 256)]
+LONG_LAST = [(0, QUARTER), (QUARTER, QUARTER), (BANK, BANK)]
+SHORT_LAST = [(0, QUARTER), (QUARTER, BANK), (BANK + QUARTER, QUARTER)]
+STEPS = {(0, 0): LONG_LAST, (0, 1): LONG_LAST, (1, 0): LONG_LAST, (1, 1): SHORT_LAST}
+PARTS = [[(0, BANK), (BANK, BANK)], [(first, QUARTER) for first in range(0, S, QUARTER)]]
+STEPS_ON_VECTOR = {(0, 0): 2, (0, 1): 2, (0, 2): 0}
+GROUPS = [(b, first) for b in range(N // P) for first in range(0, S, BANK)]
+OUTPUTS = [(0, 0, BANK), (0, BANK, BANK), (1, 0, BANK), (1, BANK, QUARTER), (1, BANK + QUARTER, QUARTER)]
+FETCHED_BY_VECTOR = OUTPUTS[-1]
 
 
 def tile_picked_sidegate_sigmoid_l_kernel(tc, xT, side, w1_words, w1_scales, offs, out):
@@ -57,7 +58,7 @@ def tile_picked_sidegate_sigmoid_l_kernel(tc, xT, side, w1_words, w1_scales, off
         nc.vector.memset(warm[:, 0:8], 0.0)
         nc.scalar.activation(out=warm[:, 8:16], in_=warm[:, 0:8], func=sigmoid)
 
-        side_rows = [keep.tile([P, T], F32, name=f"side_rows{b}") for b in range(2)]
+        side_rows = [keep.tile([P, T], F32, name=f"side_rows{b}") for b in range(N // P)]
         x_rows = xT.rearrange("(g p t) c -> g p t c", g=2, p=P, t=4)
         first_rows = keep.tile([P, 2, T], F32, name="first_rows")
         nc.sync.dma_start(out=first_rows[:], in_=x_rows[0, :, 0:2, :])
@@ -67,8 +68,8 @@ def tile_picked_sidegate_sigmoid_l_kernel(tc, xT, side, w1_words, w1_scales, off
             rows[g, t] = keep.tile([P, T], F32, name=f"row{g}_{t}")[:]
             nc.sync.dma_start(out=rows[g, t], in_=x_rows[g, :, t, :])
         nc.sync.dma_start(out=w_codes[:].bitcast(I32), in_=w1_words.rearrange("g p n -> p g n").bitcast(I32))
-        nc.sync.dma_start(out=side_rows[0][:], in_=side[0:P, :])
-        nc.sync.dma_start(out=side_rows[1][:], in_=side[P : 2 * P, :])
+        for b in range(N // P):
+            nc.sync.dma_start(out=side_rows[b][:], in_=side[b * P : (b + 1) * P, :])
 
         planes = {
             (g, u, first): keep.tile([P, 2, count], F32 if (g, u) == (0, 0) else BF16, name=f"planes{g}_{u}_{first}")
@@ -84,20 +85,20 @@ def tile_picked_sidegate_sigmoid_l_kernel(tc, xT, side, w1_words, w1_scales, off
         }
         x_codes = {(g, h): keep.tile([P, BANK], U32, name=f"x_codes{g}_{h}", align_bytes=MX_ALIGN) for g, h in halves}
         x_scales = {(g, h): keep.tile([P, BANK], U8, name=f"x_scales{g}_{h}", align_bytes=MX_ALIGN) for g, h in halves}
-        acc = {(b, first): psum.tile([P, BANK], F32, name=f"acc{b}_{first}") for b, first, count in GROUPS}
+        acc = {(b, first): psum.tile([P, BANK], F32, name=f"acc{b}_{first}") for b, first in GROUPS}
         gates = {(b, first): keep.tile([P, count], F32, name=f"gates{b}_{first}") for b, first, count in OUTPUTS}
 
         def gather_row(g, t):
             u, e = divmod(t, 2)
             for step, (first, count) in enumerate(STEPS[g, u]):
                 source = rows[g, t].indirect(entries(first, count))
-                if step < ON_VECTOR.get((g, t), 1):
+                if step < STEPS_ON_VECTOR.get((g, t), 1):
                     nc.vector.tensor_copy(out=planes[g, u, first][:, e, :], in_=source)
                 else:
                     nc.scalar.activation(out=planes[g, u, first][:, e, :], in_=source, func=mybir.ActivationFunctionType.Copy)
 
-        def place(g, u, first, count):
-            for start, width in PARTS[g]:
+        def place(g, u, start, width):
+            for first, count in STEPS[g, u]:
                 lo, hi = max(first, start), min(first + count, start + width)
                 if lo < hi:
                     nc.vector.tensor_copy(
@@ -114,7 +115,7 @@ def tile_picked_sidegate_sigmoid_l_kernel(tc, xT, side, w1_words, w1_scales, off
             )
 
         def multiply(g):
-            for b, first, count in GROUPS:
+            for b, first in GROUPS:
                 h = first // BANK
                 nc.tensor.matmul_mx(
                     out=acc[b, first][:],
@@ -128,7 +129,7 @@ def tile_picked_sidegate_sigmoid_l_kernel(tc, xT, side, w1_words, w1_scales, off
 
         def gate(b, first, count):
             source = side_rows[b][:].indirect(entries(first, count))
-            if (b, first, count) in HELPED:
+            if (b, first, count) == FETCHED_BY_VECTOR:
                 fetched = keep.tile([P, count], F32, name=f"fetched{b}_{first}")
                 nc.vector.tensor_copy(out=fetched[:], in_=source)
                 source = fetched[:]
@@ -136,10 +137,10 @@ def tile_picked_sidegate_sigmoid_l_kernel(tc, xT, side, w1_words, w1_scales, off
 
         def finish(b, first, count):
             result = keep.tile([P, count], F32, name=f"result{b}_{first}")
-            start = first // BANK * BANK
+            h, inside = divmod(first, BANK)
             nc.vector.tensor_tensor(
                 out=result[:],
-                in0=acc[b, start][:, first - start : first - start + count],
+                in0=acc[b, h * BANK][:, inside : inside + count],
                 in1=gates[b, first][:],
                 op=mybir.AluOpType.mult,
             )
@@ -148,17 +149,18 @@ def tile_picked_sidegate_sigmoid_l_kernel(tc, xT, side, w1_words, w1_scales, off
         for g in range(2):
             gather_row(g, 0)
             gather_row(g, 1)
-            for step in STEPS[g, 0]:
-                place(g, 0, *step)
+            for part in PARTS[g]:
+                place(g, 0, *part)
             gather_row(g, 2)
             gather_row(g, 3)
-            placed = 0
-            for first, count in PARTS[g]:
-                for step in STEPS[g, 1]:
-                    if placed <= step[0] <= first + count:
-                        place(g, 1, *step)
-                placed = first + count + 1
-                quantize(g, first, count)
+            head, rest = PARTS[g][0], PARTS[g][1:]
+            place(g, 1, *head)
+            quantize(g, *head)
+            place(g, 1, *rest[0])
+            for part, ahead in zip(rest, rest[1:]):
+                place(g, 1, *ahead)
+                quantize(g, *part)
+            quantize(g, *rest[-1])
             multiply(g)
 
         for piece in OUTPUTS:

@@ -15,18 +15,19 @@ FP8X4 = mybir.dt.float8_e4m3fn_x4
 FP4X4 = mybir.dt.float4_e2m1fn_x4
 
 P = 128
-BANK = 512
 LIST_ROWS = 16
 MX_ALIGN = 64
+HALF = S // 2
 QUARTER = S // 4
 
-LONG_LAST = [(0, QUARTER), (QUARTER, QUARTER), (BANK, BANK)]
-SHORT_LAST = [(0, QUARTER), (QUARTER, BANK), (BANK + QUARTER, QUARTER)]
-STEPS = {(0, 0): LONG_LAST, (0, 1): LONG_LAST, (1, 0): LONG_LAST, (1, 1): SHORT_LAST}
-PARTS = [[(0, BANK), (BANK, BANK)], [(first, QUARTER) for first in range(0, S, QUARTER)]]
-STEPS_ON_VECTOR = {(0, 0): 2, (0, 1): 2, (0, 2): 0}
-GROUPS = [(b, first) for b in range(N // P) for first in range(0, S, BANK)]
-OUTPUTS = [(0, 0, BANK), (0, BANK, BANK), (1, 0, BANK), (1, BANK, QUARTER), (1, BANK + QUARTER, QUARTER)]
+QUARTERS = [(first, QUARTER) for first in range(0, S, QUARTER)]
+HALVES = [(0, HALF), (HALF, HALF)]
+LONG_LAST = QUARTERS[:2] + HALVES[1:]
+X_LOADS = [(0, 0, 2), (0, 2, 1), (0, 3, 1), (1, 0, 1), (1, 1, 1), (1, 2, 1), (1, 3, 1)]
+STEPS = {(0, 0): LONG_LAST, (0, 1): LONG_LAST, (1, 0): LONG_LAST, (1, 1): QUARTERS}
+STEPS_ON_VECTOR = {(0, 0): 2, (0, 1): 2, (0, 2): 0, (0, 3): 1, (1, 0): 1, (1, 1): 1, (1, 2): 1, (1, 3): 1}
+GROUPS = [(0, 0, HALF), (1, 0, HALF), (0, HALF, QUARTER), (0, HALF + QUARTER, QUARTER), (1, HALF, HALF)]
+OUTPUTS = [(0, 0, HALF), (0, HALF, QUARTER), (0, HALF + QUARTER, QUARTER)] + [(1, *q) for q in QUARTERS]
 FETCHED_BY_VECTOR = OUTPUTS[-1]
 
 
@@ -58,44 +59,61 @@ def tile_picked_sidegate_sigmoid_l_kernel(tc, xT, side, w1_words, w1_scales, off
         nc.vector.memset(warm[:, 0:8], 0.0)
         nc.scalar.activation(out=warm[:, 8:16], in_=warm[:, 0:8], func=sigmoid)
 
-        side_rows = [keep.tile([P, T], F32, name=f"side_rows{b}") for b in range(N // P)]
         x_rows = xT.rearrange("(g p t) c -> g p t c", g=2, p=P, t=4)
-        first_rows = keep.tile([P, 2, T], F32, name="first_rows")
-        nc.sync.dma_start(out=first_rows[:], in_=x_rows[0, :, 0:2, :])
-        nc.sync.dma_start(offsets[:], offs)
-        rows = {(0, t): first_rows[:, t, :] for t in range(2)}
-        for g, t in [(g, t) for g in range(2) for t in range(4)][2:]:
-            rows[g, t] = keep.tile([P, T], F32, name=f"row{g}_{t}")[:]
-            nc.sync.dma_start(out=rows[g, t], in_=x_rows[g, :, t, :])
+        rows, shares_tile = {}, {}
+        for g, t, count in X_LOADS:
+            loaded = keep.tile([P, count, T] if count > 1 else [P, T], F32, name=f"rows{g}_{t}")
+            if count > 1:
+                nc.sync.dma_start(out=loaded[:], in_=x_rows[g, :, t : t + count, :])
+            else:
+                nc.sync.dma_start(out=loaded[:], in_=x_rows[g, :, t, :])
+            if (g, t) == (0, 0):
+                nc.sync.dma_start(offsets[:], offs)
+            for e in range(count):
+                rows[g, t + e] = loaded[:, e, :] if count > 1 else loaded[:]
+            shares_tile[g, t // 2] = count > 1
         nc.sync.dma_start(out=w_codes[:].bitcast(I32), in_=w1_words.rearrange("g p n -> p g n").bitcast(I32))
+        side_rows = [keep.tile([P, T], F32, name=f"side_rows{b}") for b in range(N // P)]
         for b in range(N // P):
             nc.sync.dma_start(out=side_rows[b][:], in_=side[b * P : (b + 1) * P, :])
 
         planes = {
-            (g, u, first): keep.tile([P, 2, count], F32 if (g, u) == (0, 0) else BF16, name=f"planes{g}_{u}_{first}")
+            (g, u, first): keep.tile([P, 2, count], F32 if shares_tile[g, u] else BF16, name=f"planes{g}_{u}_{first}")
             for g in range(2)
             for u in range(2)
             for first, count in STEPS[g, u]
         }
-        halves = [(g, h) for g in range(2) for h in range(S // BANK)]
+        parts = [HALVES, QUARTERS]
         woven = {
             (g, first): keep.tile([P, count, 4], BF16, name=f"woven{g}_{first}", align_bytes=MX_ALIGN)
             for g in range(2)
-            for first, count in PARTS[g]
+            for first, count in parts[g]
         }
-        x_codes = {(g, h): keep.tile([P, BANK], U32, name=f"x_codes{g}_{h}", align_bytes=MX_ALIGN) for g, h in halves}
-        x_scales = {(g, h): keep.tile([P, BANK], U8, name=f"x_scales{g}_{h}", align_bytes=MX_ALIGN) for g, h in halves}
-        acc = {(b, first): psum.tile([P, BANK], F32, name=f"acc{b}_{first}") for b, first in GROUPS}
+        halves = [(g, h) for g in range(2) for h in range(2)]
+        x_codes = {(g, h): keep.tile([P, HALF], U32, name=f"x_codes{g}_{h}", align_bytes=MX_ALIGN) for g, h in halves}
+        x_scales = {(g, h): keep.tile([P, HALF], U8, name=f"x_scales{g}_{h}", align_bytes=MX_ALIGN) for g, h in halves}
+        acc = {(b, first): psum.tile([P, count], F32, name=f"acc{b}_{first}") for b, first, count in GROUPS}
         gates = {(b, first): keep.tile([P, count], F32, name=f"gates{b}_{first}") for b, first, count in OUTPUTS}
 
-        def gather_row(g, t):
+        def gather(g, t, step):
             u, e = divmod(t, 2)
-            for step, (first, count) in enumerate(STEPS[g, u]):
-                source = rows[g, t].indirect(entries(first, count))
-                if step < STEPS_ON_VECTOR.get((g, t), 1):
-                    nc.vector.tensor_copy(out=planes[g, u, first][:, e, :], in_=source)
-                else:
-                    nc.scalar.activation(out=planes[g, u, first][:, e, :], in_=source, func=mybir.ActivationFunctionType.Copy)
+            first, count = STEPS[g, u][step]
+            source = rows[g, t].indirect(entries(first, count))
+            if step < STEPS_ON_VECTOR[g, t]:
+                nc.vector.tensor_copy(out=planes[g, u, first][:, e, :], in_=source)
+            else:
+                nc.scalar.activation(out=planes[g, u, first][:, e, :], in_=source, func=mybir.ActivationFunctionType.Copy)
+
+        def gather_pair(g, u):
+            steps = range(len(STEPS[g, u]))
+            if shares_tile[g, u]:
+                for step in steps:
+                    gather(g, 2 * u, step)
+                    gather(g, 2 * u + 1, step)
+            else:
+                for t in (2 * u, 2 * u + 1):
+                    for step in steps:
+                        gather(g, t, step)
 
         def place(g, u, start, width):
             for first, count in STEPS[g, u]:
@@ -107,7 +125,7 @@ def tile_picked_sidegate_sigmoid_l_kernel(tc, xT, side, w1_words, w1_scales, off
                     )
 
         def quantize(g, first, count):
-            h, inside = divmod(first, BANK)
+            h, inside = divmod(first, HALF)
             nc.vector.quantize_mx(
                 out=x_codes[g, h][:, inside : inside + count].bitcast(FP8X4),
                 scales=x_scales[g, h][:, inside : inside + count],
@@ -115,14 +133,14 @@ def tile_picked_sidegate_sigmoid_l_kernel(tc, xT, side, w1_words, w1_scales, off
             )
 
         def multiply(g):
-            for b, first in GROUPS:
-                h = first // BANK
+            for b, first, count in GROUPS:
+                h, inside = divmod(first, HALF)
                 nc.tensor.matmul_mx(
                     out=acc[b, first][:],
                     lhsT=w_codes[:, g, 2 * P * b : 2 * P * (b + 1)].bitcast(FP4X4),
                     lhsT_scale=w_scales[:, g, P * b : P * (b + 1)],
-                    rhs=x_codes[g, h][:].bitcast(FP8X4),
-                    rhs_scale=x_scales[g, h][:],
+                    rhs=x_codes[g, h][:, inside : inside + count].bitcast(FP8X4),
+                    rhs_scale=x_scales[g, h][:, inside : inside + count],
                     start=(g == 0),
                     stop=(g == 1),
                 )
@@ -137,31 +155,36 @@ def tile_picked_sidegate_sigmoid_l_kernel(tc, xT, side, w1_words, w1_scales, off
 
         def finish(b, first, count):
             result = keep.tile([P, count], F32, name=f"result{b}_{first}")
-            h, inside = divmod(first, BANK)
+            start = max(s for c, s, n in GROUPS if c == b and s <= first)
             nc.vector.tensor_tensor(
                 out=result[:],
-                in0=acc[b, h * BANK][:, inside : inside + count],
+                in0=acc[b, start][:, first - start : first - start + count],
                 in1=gates[b, first][:],
                 op=mybir.AluOpType.mult,
             )
             nc.sync.dma_start(out=out[P * b : P * (b + 1), first : first + count], in_=result[:])
 
-        for g in range(2):
-            gather_row(g, 0)
-            gather_row(g, 1)
-            for part in PARTS[g]:
-                place(g, 0, *part)
-            gather_row(g, 2)
-            gather_row(g, 3)
-            head, rest = PARTS[g][0], PARTS[g][1:]
-            place(g, 1, *head)
-            quantize(g, *head)
-            place(g, 1, *rest[0])
-            for part, ahead in zip(rest, rest[1:]):
-                place(g, 1, *ahead)
-                quantize(g, *part)
-            quantize(g, *rest[-1])
-            multiply(g)
+        gather_pair(0, 0)
+        for part in HALVES:
+            place(0, 0, *part)
+        gather_pair(0, 1)
+        for part in HALVES:
+            place(0, 1, *part)
+        for part in HALVES:
+            quantize(0, *part)
+        multiply(0)
+
+        gather_pair(1, 0)
+        for part in QUARTERS:
+            place(1, 0, *part)
+        gather_pair(1, 1)
+        order = [QUARTERS[1], QUARTERS[0]] + QUARTERS[2:]
+        place(1, 1, *order[0])
+        for part, ahead in zip(order, order[1:]):
+            place(1, 1, *ahead)
+            quantize(1, *part)
+        quantize(1, *order[-1])
+        multiply(1)
 
         for piece in OUTPUTS:
             gate(*piece)

@@ -22,13 +22,14 @@ QUARTER = S // 4
 
 QUARTERS = [(first, QUARTER) for first in range(0, S, QUARTER)]
 HALVES = [(0, HALF), (HALF, HALF)]
-LONG_LAST = QUARTERS[:2] + HALVES[1:]
 X_LOADS = [(0, 0, 2), (0, 2, 1), (0, 3, 1), (1, 0, 1), (1, 1, 1), (1, 2, 1), (1, 3, 1)]
-STEPS = {(0, 0): LONG_LAST, (0, 1): LONG_LAST, (1, 0): LONG_LAST, (1, 1): QUARTERS}
-STEPS_ON_VECTOR = {(0, 0): 2, (0, 1): 2, (0, 2): 0, (0, 3): 1, (1, 0): 1, (1, 1): 1, (1, 2): 1, (1, 3): 1}
-GROUPS = [(0, 0, HALF), (1, 0, HALF), (0, HALF, QUARTER), (0, HALF + QUARTER, QUARTER), (1, HALF, HALF)]
-OUTPUTS = [(0, 0, HALF), (0, HALF, QUARTER), (0, HALF + QUARTER, QUARTER)] + [(1, *q) for q in QUARTERS]
-FETCHED_BY_VECTOR = OUTPUTS[-1]
+ON_VECTOR = {(0, 0): HALF, (0, 1): HALF, (0, 2): 0, (0, 3): HALF, (1, 0): 0, (1, 1): HALF, (1, 2): QUARTER, (1, 3): QUARTER}
+LAST_ROW = (1, 3)
+GROUPS = [(b, *half) for b in range(N // P) for half in HALVES]
+GATES = [(0, 0, S - QUARTER), (0, *QUARTERS[-1]), (1, *HALVES[0])] + [(1, *q) for q in QUARTERS[2:]]
+FETCHED_BY_VECTOR = [(b, *QUARTERS[-1]) for b in range(N // P)]
+OUTPUTS = [(0, *half) for half in HALVES] + GATES[-3:]
+PLACED_BY_SCALAR = 128
 
 
 def tile_picked_sidegate_sigmoid_l_kernel(tc, xT, side, w1_words, w1_scales, offs, out):
@@ -78,10 +79,9 @@ def tile_picked_sidegate_sigmoid_l_kernel(tc, xT, side, w1_words, w1_scales, off
             nc.sync.dma_start(out=side_rows[b][:], in_=side[b * P : (b + 1) * P, :])
 
         planes = {
-            (g, u, first): keep.tile([P, 2, count], F32 if shares_tile[g, u] else BF16, name=f"planes{g}_{u}_{first}")
+            (g, u): keep.tile([P, 2, S], F32 if shares_tile[g, u] else BF16, name=f"planes{g}_{u}")
             for g in range(2)
             for u in range(2)
-            for first, count in STEPS[g, u]
         }
         parts = [HALVES, QUARTERS]
         woven = {
@@ -93,36 +93,32 @@ def tile_picked_sidegate_sigmoid_l_kernel(tc, xT, side, w1_words, w1_scales, off
         x_codes = {(g, h): keep.tile([P, HALF], U32, name=f"x_codes{g}_{h}", align_bytes=MX_ALIGN) for g, h in halves}
         x_scales = {(g, h): keep.tile([P, HALF], U8, name=f"x_scales{g}_{h}", align_bytes=MX_ALIGN) for g, h in halves}
         acc = {(b, first): psum.tile([P, count], F32, name=f"acc{b}_{first}") for b, first, count in GROUPS}
-        gates = {(b, first): keep.tile([P, count], F32, name=f"gates{b}_{first}") for b, first, count in OUTPUTS}
+        gates = [keep.tile([P, S], F32, name=f"gates{b}") for b in range(N // P)]
 
-        def gather(g, t, step):
+        def gather(g, t):
             u, e = divmod(t, 2)
-            first, count = STEPS[g, u][step]
-            source = rows[g, t].indirect(entries(first, count))
-            if step < STEPS_ON_VECTOR[g, t]:
-                nc.vector.tensor_copy(out=planes[g, u, first][:, e, :], in_=source)
-            else:
-                nc.scalar.activation(out=planes[g, u, first][:, e, :], in_=source, func=mybir.ActivationFunctionType.Copy)
+            cut = ON_VECTOR[g, t]
+            if cut:
+                nc.vector.tensor_copy(out=planes[g, u][:, e, :cut], in_=rows[g, t].indirect(entries(0, cut)))
+            steps = [QUARTERS[1], HALVES[1]] if (g, t) == LAST_ROW else [(cut, S - cut)]
+            for first, count in steps:
+                nc.scalar.activation(
+                    out=planes[g, u][:, e, first : first + count],
+                    in_=rows[g, t].indirect(entries(first, count)),
+                    func=mybir.ActivationFunctionType.Copy,
+                )
 
         def gather_pair(g, u):
-            steps = range(len(STEPS[g, u]))
-            if shares_tile[g, u]:
-                for step in steps:
-                    gather(g, 2 * u, step)
-                    gather(g, 2 * u + 1, step)
-            else:
-                for t in (2 * u, 2 * u + 1):
-                    for step in steps:
-                        gather(g, t, step)
+            gather(g, 2 * u)
+            gather(g, 2 * u + 1)
 
-        def place(g, u, start, width):
-            for first, count in STEPS[g, u]:
-                lo, hi = max(first, start), min(first + count, start + width)
-                if lo < hi:
-                    nc.vector.tensor_copy(
-                        out=woven[g, start][:, lo - start : hi - start, 2 * u : 2 * u + 2],
-                        in_=planes[g, u, first][:, :, lo - first : hi - first].rearrange("p e j -> p j e"),
-                    )
+        def place(g, u, first, count):
+            cut = count - PLACED_BY_SCALAR if (g, u, first + count) == (1, 1, S) else count
+            source = planes[g, u][:, :, first : first + count].rearrange("p e j -> p j e")
+            target = woven[g, first][:, :, 2 * u : 2 * u + 2]
+            nc.vector.tensor_copy(out=target[:, :cut, :], in_=source[:, :cut, :])
+            if cut < count:
+                nc.scalar.copy(out=target[:, cut:, :], in_=source[:, cut:, :])
 
         def quantize(g, first, count):
             h, inside = divmod(first, HALF)
@@ -147,11 +143,11 @@ def tile_picked_sidegate_sigmoid_l_kernel(tc, xT, side, w1_words, w1_scales, off
 
         def gate(b, first, count):
             source = side_rows[b][:].indirect(entries(first, count))
-            if (b, first, count) == FETCHED_BY_VECTOR:
+            if (b, first, count) in FETCHED_BY_VECTOR:
                 fetched = keep.tile([P, count], F32, name=f"fetched{b}_{first}")
                 nc.vector.tensor_copy(out=fetched[:], in_=source)
                 source = fetched[:]
-            nc.scalar.activation(out=gates[b, first][:], in_=source, func=sigmoid)
+            nc.scalar.activation(out=gates[b][:, first : first + count], in_=source, func=sigmoid)
 
         def finish(b, first, count):
             result = keep.tile([P, count], F32, name=f"result{b}_{first}")
@@ -159,7 +155,7 @@ def tile_picked_sidegate_sigmoid_l_kernel(tc, xT, side, w1_words, w1_scales, off
             nc.vector.tensor_tensor(
                 out=result[:],
                 in0=acc[b, start][:, first - start : first - start + count],
-                in1=gates[b, first][:],
+                in1=gates[b][:, first : first + count],
                 op=mybir.AluOpType.mult,
             )
             nc.sync.dma_start(out=out[P * b : P * (b + 1), first : first + count], in_=result[:])
@@ -178,15 +174,14 @@ def tile_picked_sidegate_sigmoid_l_kernel(tc, xT, side, w1_words, w1_scales, off
         for part in QUARTERS:
             place(1, 0, *part)
         gather_pair(1, 1)
-        order = [QUARTERS[1], QUARTERS[0]] + QUARTERS[2:]
-        place(1, 1, *order[0])
-        for part, ahead in zip(order, order[1:]):
-            place(1, 1, *ahead)
-            quantize(1, *part)
-        quantize(1, *order[-1])
+        for both in (QUARTERS[1::-1], QUARTERS[2:]):
+            for part in both:
+                place(1, 1, *part)
+            for part in both:
+                quantize(1, *part)
         multiply(1)
 
-        for piece in OUTPUTS:
+        for piece in GATES:
             gate(*piece)
         for piece in OUTPUTS:
             finish(*piece)

@@ -28,7 +28,7 @@ LAST_ROW = (1, 3)
 GROUPS = [(b, *half) for b in range(N // P) for half in HALVES]
 GATES = [(0, 0, S - QUARTER), (0, *QUARTERS[-1]), (1, *HALVES[0])] + [(1, *q) for q in QUARTERS[2:]]
 FETCHED_BY_VECTOR = [(b, *QUARTERS[-1]) for b in range(N // P)]
-OUTPUTS = [(0, *half) for half in HALVES] + GATES[-3:]
+OUTPUTS = [(0, *half) for half in HALVES] + [(1, *q) for q in QUARTERS]
 PLACED_BY_SCALAR = 128
 
 

@@ -25,11 +25,12 @@ HALVES = [(0, HALF), (HALF, HALF)]
 X_LOADS = [(0, 0, 2), (0, 2, 1), (0, 3, 1), (1, 0, 1), (1, 1, 1), (1, 2, 1), (1, 3, 1)]
 ON_VECTOR = {(0, 0): HALF, (0, 1): HALF, (0, 2): 0, (0, 3): HALF, (1, 0): 0, (1, 1): HALF, (1, 2): QUARTER, (1, 3): QUARTER}
 LAST_ROW = (1, 3)
+LAST_PAIR = (1, 1)
 GROUPS = [(b, *half) for b in range(N // P) for half in HALVES]
-GATES = [(0, 0, S - QUARTER), (0, *QUARTERS[-1]), (1, *HALVES[0])] + [(1, *q) for q in QUARTERS[2:]]
+GATES = [(b, *part) for b in range(N // P) for part in HALVES[:1] + QUARTERS[2:]]
 FETCHED_BY_VECTOR = [(b, *QUARTERS[-1]) for b in range(N // P)]
-OUTPUTS = [(0, *half) for half in HALVES] + [(1, *q) for q in QUARTERS]
-PLACED_BY_SCALAR = 128
+OUTPUTS = GATES[:3] + [(1, *q) for q in QUARTERS]
+PLACED_BY_SCALAR = {(1, 0): QUARTER}
 
 
 def tile_picked_sidegate_sigmoid_l_kernel(tc, xT, side, w1_words, w1_scales, offs, out):
@@ -99,8 +100,9 @@ def tile_picked_sidegate_sigmoid_l_kernel(tc, xT, side, w1_words, w1_scales, off
             u, e = divmod(t, 2)
             cut = ON_VECTOR[g, t]
             if cut:
-                nc.vector.tensor_copy(out=planes[g, u][:, e, :cut], in_=rows[g, t].indirect(entries(0, cut)))
-            steps = [QUARTERS[1], HALVES[1]] if (g, t) == LAST_ROW else [(cut, S - cut)]
+                target = woven[g, 0][:, :, t] if (g, u) == LAST_PAIR else planes[g, u][:, e, :cut]
+                nc.vector.tensor_copy(out=target, in_=rows[g, t].indirect(entries(0, cut)))
+            steps = QUARTERS[1:] if (g, t) == LAST_ROW else [(cut, S - cut)]
             for first, count in steps:
                 nc.scalar.activation(
                     out=planes[g, u][:, e, first : first + count],
@@ -113,10 +115,11 @@ def tile_picked_sidegate_sigmoid_l_kernel(tc, xT, side, w1_words, w1_scales, off
             gather(g, 2 * u + 1)
 
         def place(g, u, first, count):
-            cut = count - PLACED_BY_SCALAR if (g, u, first + count) == (1, 1, S) else count
+            cut = count - PLACED_BY_SCALAR.get((g, u), 0) if first + count == S else count
             source = planes[g, u][:, :, first : first + count].rearrange("p e j -> p j e")
             target = woven[g, first][:, :, 2 * u : 2 * u + 2]
-            nc.vector.tensor_copy(out=target[:, :cut, :], in_=source[:, :cut, :])
+            if cut:
+                nc.vector.tensor_copy(out=target[:, :cut, :], in_=source[:, :cut, :])
             if cut < count:
                 nc.scalar.copy(out=target[:, cut:, :], in_=source[:, cut:, :])
 
@@ -174,11 +177,10 @@ def tile_picked_sidegate_sigmoid_l_kernel(tc, xT, side, w1_words, w1_scales, off
         for part in QUARTERS:
             place(1, 0, *part)
         gather_pair(1, 1)
-        for both in (QUARTERS[1::-1], QUARTERS[2:]):
-            for part in both:
-                place(1, 1, *part)
-            for part in both:
-                quantize(1, *part)
+        for part, ahead in zip(QUARTERS, QUARTERS[1:]):
+            place(1, 1, *ahead)
+            quantize(1, *part)
+        quantize(1, *QUARTERS[-1])
         multiply(1)
 
         for piece in GATES:

@@ -41,7 +41,7 @@ def tile_picked_sidegate_sigmoid_l_kernel(tc, xT, side, w1_words, w1_scales, off
         psum = ctx.enter_context(tc.psum_pool(name="psum", bufs=1))
 
         offsets = keep.tile([P, S // LIST_ROWS], U16, name="offsets")
-        w_codes = keep.tile([P, 2, 2 * N], U8, name="w_codes", align_bytes=MX_ALIGN)
+        w_codes = [keep.tile([P, 2 * N], U8, name=f"w_codes{g}", align_bytes=MX_ALIGN) for g in range(2)]
         w_scales = keep.tile([P, 2, N], U8, name="w_scales", align_bytes=MX_ALIGN)
         scale_rows = keep.tile([P, 2, N], U8, name="scale_rows")
 
@@ -74,9 +74,9 @@ def tile_picked_sidegate_sigmoid_l_kernel(tc, xT, side, w1_words, w1_scales, off
             for e in range(count):
                 rows[g, t + e] = loaded[:, e, :] if count > 1 else loaded[:]
             shares_tile[g, t // 2] = count > 1
-        nc.sync.dma_start(out=w_codes[:].bitcast(I32), in_=w1_words.rearrange("g p n -> p g n").bitcast(I32))
         side_rows = [keep.tile([P, T], F32, name=f"side_rows{b}") for b in range(N // P)]
         for b in range(N // P):
+            nc.sync.dma_start(out=w_codes[b][:].bitcast(I32), in_=w1_words[b].bitcast(I32))
             nc.sync.dma_start(out=side_rows[b][:], in_=side[b * P : (b + 1) * P, :])
 
         planes = {
@@ -136,7 +136,7 @@ def tile_picked_sidegate_sigmoid_l_kernel(tc, xT, side, w1_words, w1_scales, off
                 h, inside = divmod(first, HALF)
                 nc.tensor.matmul_mx(
                     out=acc[b, first][:],
-                    lhsT=w_codes[:, g, 2 * P * b : 2 * P * (b + 1)].bitcast(FP4X4),
+                    lhsT=w_codes[g][:, 2 * P * b : 2 * P * (b + 1)].bitcast(FP4X4),
                     lhsT_scale=w_scales[:, g, P * b : P * (b + 1)],
                     rhs=x_codes[g, h][:, inside : inside + count].bitcast(FP8X4),
                     rhs_scale=x_scales[g, h][:, inside : inside + count],

@@ -27,9 +27,9 @@ ON_VECTOR = {(0, 0): HALF, (0, 1): HALF, (0, 2): 0, (0, 3): HALF, (1, 0): 0, (1,
 LAST_ROW = (1, 3)
 LAST_PAIR = (1, 1)
 GROUPS = [(b, *half) for b in range(N // P) for half in HALVES]
-GATES = [(b, *part) for b in range(N // P) for part in HALVES[:1] + QUARTERS[2:]]
-FETCHED_BY_VECTOR = [(b, *QUARTERS[-1]) for b in range(N // P)]
-OUTPUTS = GATES[:3] + [(1, *q) for q in QUARTERS]
+GATES = [(0, *part) for part in [(0, 512), (512, 320), (832, 192)]] + [(1, *part) for part in QUARTERS[:3] + [(768, 128), (896, 128)]]
+FETCHED_BY_VECTOR = [(0, *part) for part in [(832, 192)]] + [(1, *part) for part in [(768, 256)]]
+OUTPUTS = [(0, *part) for part in [(0, 512), (512, 320), (832, 192)]] + [(1, *part) for part in QUARTERS[:3] + [(768, 128), (896, 128)]]
 PLACED_BY_SCALAR = {(1, 0): QUARTER}
 
 
@@ -144,12 +144,18 @@ def tile_picked_sidegate_sigmoid_l_kernel(tc, xT, side, w1_words, w1_scales, off
                     stop=(g == 1),
                 )
 
+        fetched = {}
+
+        def fetch(b, first, count):
+            fetched[b] = first, keep.tile([P, count], F32, name=f"fetched{b}")
+            nc.vector.tensor_copy(out=fetched[b][1][:], in_=side_rows[b][:].indirect(entries(first, count)))
+
         def gate(b, first, count):
-            source = side_rows[b][:].indirect(entries(first, count))
-            if (b, first, count) in FETCHED_BY_VECTOR:
-                fetched = keep.tile([P, count], F32, name=f"fetched{b}_{first}")
-                nc.vector.tensor_copy(out=fetched[:], in_=source)
-                source = fetched[:]
+            start, values = fetched[b]
+            if first >= start:
+                source = values[:, first - start : first - start + count]
+            else:
+                source = side_rows[b][:].indirect(entries(first, count))
             nc.scalar.activation(out=gates[b][:, first : first + count], in_=source, func=sigmoid)
 
         def finish(b, first, count):
@@ -183,6 +189,8 @@ def tile_picked_sidegate_sigmoid_l_kernel(tc, xT, side, w1_words, w1_scales, off
         quantize(1, *QUARTERS[-1])
         multiply(1)
 
+        for piece in FETCHED_BY_VECTOR:
+            fetch(*piece)
         for piece in GATES:
             gate(*piece)
         for piece in OUTPUTS:

@@ -27,9 +27,9 @@ ON_VECTOR = {(0, 0): HALF, (0, 1): HALF, (0, 2): 0, (0, 3): HALF, (1, 0): 0, (1,
 LAST_ROW = (1, 3)
 LAST_PAIR = (1, 1)
 GROUPS = [(b, *half) for b in range(N // P) for half in HALVES]
-GATES = [(0, *part) for part in [(0, 512), (512, 320), (832, 192)]] + [(1, *part) for part in QUARTERS[:3] + [(768, 128), (896, 128)]]
-FETCHED_BY_VECTOR = [(0, *part) for part in [(832, 192)]] + [(1, *part) for part in [(768, 256)]]
-OUTPUTS = [(0, *part) for part in [(0, 512), (512, 320), (832, 192)]] + [(1, *part) for part in QUARTERS[:3] + [(768, 128), (896, 128)]]
+GATES = [(0, *part) for part in [(0, 512), (512, 320), (832, 192)]] + [(1, *part) for part in [(0, 256), (256, 256), (512, 192), (704, 192), (896, 128)]]
+FETCHED_BY_VECTOR = [(0, *part) for part in [(832, 192)]] + [(1, *part) for part in [(704, 320)]]
+OUTPUTS = [(0, *part) for part in [(0, 512), (512, 320), (832, 192)]] + [(1, *part) for part in [(0, 256), (256, 256), (512, 192), (704, 192), (896, 128)]]
 PLACED_BY_SCALAR = {(1, 0): QUARTER}
 
 

from contextlib import ExitStack

import concourse.mybir as mybir

K, T, S, N = 1024, 2048, 1024, 256
FLOPS = 2 * K * S * N

F32 = mybir.dt.float32
BF16 = mybir.dt.bfloat16
I32 = mybir.dt.int32
U32 = mybir.dt.uint32
U16 = mybir.dt.uint16
U8 = mybir.dt.uint8
FP8X4 = mybir.dt.float8_e4m3fn_x4
FP4X4 = mybir.dt.float4_e2m1fn_x4

P = 128
LIST_ROWS = 16
MX_ALIGN = 64
HALF = S // 2
QUARTER = S // 4

QUARTERS = [(first, QUARTER) for first in range(0, S, QUARTER)]
HALVES = [(0, HALF), (HALF, HALF)]
X_LOADS = [(0, 0, 2), (0, 2, 1), (0, 3, 1), (1, 0, 1), (1, 1, 1), (1, 2, 1), (1, 3, 1)]
ON_VECTOR = {(0, 0): HALF, (0, 1): HALF, (0, 2): 0, (0, 3): HALF, (1, 0): 0, (1, 1): HALF, (1, 2): QUARTER, (1, 3): QUARTER}
LAST_ROW = (1, 3)
LAST_PAIR = (1, 1)
GROUPS = [(b, *half) for b in range(N // P) for half in HALVES]
GATES = [(0, *part) for part in [(0, 512), (512, 320), (832, 192)]] + [(1, *part) for part in [(0, 256), (256, 256), (512, 192), (704, 192), (896, 128)]]
FETCHED_BY_VECTOR = [(0, *part) for part in [(832, 192)]] + [(1, *part) for part in [(704, 320)]]
OUTPUTS = [(0, *part) for part in [(0, 512), (512, 320), (832, 192)]] + [(1, *part) for part in [(0, 256), (256, 256), (512, 192), (704, 192), (896, 128)]]
PLACED_BY_SCALAR = {(1, 0): QUARTER}


def tile_picked_sidegate_sigmoid_l_kernel(tc, xT, side, w1_words, w1_scales, offs, out):
    nc = tc.nc
    sigmoid = mybir.ActivationFunctionType.Sigmoid
    with ExitStack() as ctx:
        keep = ctx.enter_context(tc.tile_pool(name="keep", bufs=1))
        psum = ctx.enter_context(tc.psum_pool(name="psum", bufs=1))

        offsets = keep.tile([P, S // LIST_ROWS], U16, name="offsets")
        w_codes = [keep.tile([P, 2 * N], U8, name=f"w_codes{g}", align_bytes=MX_ALIGN) for g in range(2)]
        w_scales = keep.tile([P, 2, N], U8, name="w_scales", align_bytes=MX_ALIGN)
        scale_rows = keep.tile([P, 2, N], U8, name="scale_rows")

        def entries(first, count):
            return offsets[:, first // LIST_ROWS : (first + count) // LIST_ROWS]

        nc.gpsimd.memset(w_scales[:].rearrange("p g n -> p (g n)").bitcast(I32), 0)
        for q in range(4):
            live = slice(32 * q, 32 * q + 4)
            nc.scalar.dma_start(
                out=scale_rows[live, :, :].bitcast(I32),
                in_=w1_scales[:, 4 * q : 4 * q + 4, :].rearrange("g r n -> r g n").bitcast(I32),
            )
            nc.gpsimd.tensor_copy(out=w_scales[live, :, :].bitcast(I32), in_=scale_rows[live, :, :].bitcast(I32))

        warm = keep.tile([P, 16], F32, name="warm")
        nc.vector.memset(warm[:, 0:8], 0.0)
        nc.scalar.activation(out=warm[:, 8:16], in_=warm[:, 0:8], func=sigmoid)

        x_rows = xT.rearrange("(g p t) c -> g p t c", g=2, p=P, t=4)
        rows, shares_tile = {}, {}
        for g, t, count in X_LOADS:
            loaded = keep.tile([P, count, T] if count > 1 else [P, T], F32, name=f"rows{g}_{t}")
            if count > 1:
                nc.sync.dma_start(out=loaded[:], in_=x_rows[g, :, t : t + count, :])
            else:
                nc.sync.dma_start(out=loaded[:], in_=x_rows[g, :, t, :])
            if (g, t) == (0, 0):
                nc.sync.dma_start(offsets[:], offs)
            for e in range(count):
                rows[g, t + e] = loaded[:, e, :] if count > 1 else loaded[:]
            shares_tile[g, t // 2] = count > 1
        side_rows = [keep.tile([P, T], F32, name=f"side_rows{b}") for b in range(N // P)]
        for b in range(N // P):
            nc.sync.dma_start(out=w_codes[b][:].bitcast(I32), in_=w1_words[b].bitcast(I32))
            nc.sync.dma_start(out=side_rows[b][:], in_=side[b * P : (b + 1) * P, :])

        planes = {
            (g, u): keep.tile([P, 2, S], F32 if shares_tile[g, u] else BF16, name=f"planes{g}_{u}")
            for g in range(2)
            for u in range(2)
        }
        parts = [HALVES, QUARTERS]
        woven = {
            (g, first): keep.tile([P, count, 4], BF16, name=f"woven{g}_{first}", align_bytes=MX_ALIGN)
            for g in range(2)
            for first, count in parts[g]
        }
        halves = [(g, h) for g in range(2) for h in range(2)]
        x_codes = {(g, h): keep.tile([P, HALF], U32, name=f"x_codes{g}_{h}", align_bytes=MX_ALIGN) for g, h in halves}
        x_scales = {(g, h): keep.tile([P, HALF], U8, name=f"x_scales{g}_{h}", align_bytes=MX_ALIGN) for g, h in halves}
        acc = {(b, first): psum.tile([P, count], F32, name=f"acc{b}_{first}") for b, first, count in GROUPS}
        gates = [keep.tile([P, S], F32, name=f"gates{b}") for b in range(N // P)]

        def gather(g, t):
            u, e = divmod(t, 2)
            cut = ON_VECTOR[g, t]
            if cut:
                target = woven[g, 0][:, :, t] if (g, u) == LAST_PAIR else planes[g, u][:, e, :cut]
                nc.vector.tensor_copy(out=target, in_=rows[g, t].indirect(entries(0, cut)))
            steps = QUARTERS[1:] if (g, t) == LAST_ROW else [(cut, S - cut)]
            for first, count in steps:
                nc.scalar.activation(
                    out=planes[g, u][:, e, first : first + count],
                    in_=rows[g, t].indirect(entries(first, count)),
                    func=mybir.ActivationFunctionType.Copy,
                )

        def gather_pair(g, u):
            gather(g, 2 * u)
            gather(g, 2 * u + 1)

        def place(g, u, first, count):
            cut = count - PLACED_BY_SCALAR.get((g, u), 0) if first + count == S else count
            source = planes[g, u][:, :, first : first + count].rearrange("p e j -> p j e")
            target = woven[g, first][:, :, 2 * u : 2 * u + 2]
            if cut:
                nc.vector.tensor_copy(out=target[:, :cut, :], in_=source[:, :cut, :])
            if cut < count:
                nc.scalar.copy(out=target[:, cut:, :], in_=source[:, cut:, :])

        def quantize(g, first, count):
            h, inside = divmod(first, HALF)
            nc.vector.quantize_mx(
                out=x_codes[g, h][:, inside : inside + count].bitcast(FP8X4),
                scales=x_scales[g, h][:, inside : inside + count],
                in_=woven[g, first][:].rearrange("p j t -> p (j t)"),
            )

        def multiply(g):
            for b, first, count in GROUPS:
                h, inside = divmod(first, HALF)
                nc.tensor.matmul_mx(
                    out=acc[b, first][:],
                    lhsT=w_codes[g][:, 2 * P * b : 2 * P * (b + 1)].bitcast(FP4X4),
                    lhsT_scale=w_scales[:, g, P * b : P * (b + 1)],
                    rhs=x_codes[g, h][:, inside : inside + count].bitcast(FP8X4),
                    rhs_scale=x_scales[g, h][:, inside : inside + count],
                    start=(g == 0),
                    stop=(g == 1),
                )

        fetched = {}

        def fetch(b, first, count):
            fetched[b] = first, keep.tile([P, count], F32, name=f"fetched{b}")
            nc.vector.tensor_copy(out=fetched[b][1][:], in_=side_rows[b][:].indirect(entries(first, count)))

        def gate(b, first, count):
            start, values = fetched[b]
            if first >= start:
                source = values[:, first - start : first - start + count]
            else:
                source = side_rows[b][:].indirect(entries(first, count))
            nc.scalar.activation(out=gates[b][:, first : first + count], in_=source, func=sigmoid)

        def finish(b, first, count):
            result = keep.tile([P, count], F32, name=f"result{b}_{first}")
            start = max(s for c, s, n in GROUPS if c == b and s <= first)
            nc.vector.tensor_tensor(
                out=result[:],
                in0=acc[b, start][:, first - start : first - start + count],
                in1=gates[b][:, first : first + count],
                op=mybir.AluOpType.mult,
            )
            nc.sync.dma_start(out=out[P * b : P * (b + 1), first : first + count], in_=result[:])

        gather_pair(0, 0)
        for part in HALVES:
            place(0, 0, *part)
        gather_pair(0, 1)
        for part in HALVES:
            place(0, 1, *part)
        for part in HALVES:
            quantize(0, *part)
        multiply(0)

        gather_pair(1, 0)
        for part in QUARTERS:
            place(1, 0, *part)
        gather_pair(1, 1)
        for part, ahead in zip(QUARTERS, QUARTERS[1:]):
            place(1, 1, *ahead)
            quantize(1, *part)
        quantize(1, *QUARTERS[-1])
        multiply(1)

        for piece in FETCHED_BY_VECTOR:
            fetch(*piece)
        for piece in GATES:
            gate(*piece)
        for piece in OUTPUTS:
            finish(*piece)
